import numpy as np
import ml_dtypes


def mxq(x, axis, fmt="e4m3"):
    dtype, down = {"e4m3": (ml_dtypes.float8_e4m3fn, 7), "e5m2": (ml_dtypes.float8_e5m2, 14)}[fmt]
    v = np.moveaxis(np.asarray(x, np.float32).astype(ml_dtypes.bfloat16).astype(np.float64), axis, -1)
    blocks = v.reshape(v.shape[:-1] + (-1, 32))
    amax = np.abs(blocks).max(-1, keepdims=True)
    byte = np.maximum(np.where(amax > 0, np.frexp(amax)[1] - 1 + 127, 0) - down, 1)
    scale = np.exp2(byte - 127.0)
    codes = (blocks / scale).astype(np.float32).astype(dtype).astype(np.float64)
    return np.moveaxis((codes * scale).reshape(v.shape), -1, axis)


WIDE = False


def mx_kscale(k):
    if not WIDE:
        return np.ones(k)
    levels = np.array([18, -18])
    if k % 512:
        return np.exp2(np.random.permutation(np.resize(levels, k // 32))).repeat(32)
    a = np.empty((k // 512, 16))
    for p in range(k // 512):
        a[p, :8] = np.random.permutation(np.resize(levels, 8))
        for g in range(8):
            far = levels[np.abs(levels - a[p, g]) >= 10]
            a[p, g + 8] = far[np.random.randint(len(far))]
    return np.exp2(a.ravel()).repeat(32)


def f64(x):
    return np.asarray(x).astype(np.float64)


def striped(idx):
    return np.tile(np.asarray(idx).reshape(-1, 16).T, (8, 1)).astype(np.uint16)


def unstriped(offs):
    return offs[:16].T.reshape(-1).astype(np.int64)

def planes(y):
    n, m = y.shape
    v = y.astype(np.float32).astype(ml_dtypes.bfloat16).astype(np.float64).reshape(n // 32, 32, m)
    top = np.abs(v).max(1)
    byte = np.clip(np.where(top > 0, np.frexp(top)[1] - 1 + 127 - 7, 1), 1, 254)
    codes = (v * np.exp2(127.0 - byte)[:, None, :]).reshape(n, m).astype(np.float32).astype(ml_dtypes.float8_e4m3fn).view(np.uint8)
    words = codes.reshape(n // 512, 128, 4, m).transpose(0, 1, 3, 2)
    return np.ascontiguousarray(words), np.ascontiguousarray(byte.astype(np.uint8).reshape(n // 512, 16, m))


B, N, T, D, R = 1, 512, 2048, 512, 512


def setup_inputs():
    n = np.random.standard_normal
    idx = np.random.permutation(T)[:B * N]
    s = mx_kscale(D)[:, None]
    z = mx_kscale(R)[:, None]
    q = n((B, D, R))
    do = n((B, D, R))
    return {
        "qT": (q * s).astype(np.float32),
        "cT": (n((D, T)) * (1.00 / np.sqrt(D)) / s).astype(np.float32),
        "doT": (do * s).astype(np.float32),
        "rw": (np.random.uniform(0.5, 1.5, (B, R, 1)) * 1.0 / np.sqrt(R) * z).astype(np.float32),
        "qm": (q.transpose(0, 2, 1) / z).astype(np.float32),
        "dom": (do.transpose(0, 2, 1) / z).astype(np.float32),
        "offs": striped(idx),
    }


def reference(qT, cT, doT, rw, qm, dom, offs):
    idx = unstriped(offs)
    pick = lambda x: x[:, idx].reshape(x.shape[0], B, N).transpose(1, 0, 2)
    cq = mxq(pick(f64(cT)), 1, "e4m3")
    a = mxq(f64(qT), 1, "e4m3").transpose(0, 2, 1) @ cq
    p = 1.0 / (1.0 + np.exp(-a))
    dp = mxq(f64(doT), 1, "e5m2").transpose(0, 2, 1) @ cq
    ds = f64(rw) * dp * p * (1.0 - p)
    dk = mxq(f64(qm), 1, "e4m3").transpose(0, 2, 1) @ mxq(ds, 1, "e5m2")
    dv = mxq(f64(dom), 1, "e5m2").transpose(0, 2, 1) @ mxq(f64(rw) * p, 1, "e4m3")
    gc = np.zeros((D, T))
    gc[:, idx] = (dk + dv).transpose(1, 0, 2).reshape(D, B * N)
    out_0 = gc
    return (out_0,) + planes(out_0)

@@ -1,0 +1,205 @@
+from contextlib import ExitStack
+
+import concourse.mybir as mybir
+
+N, T, D, R = 512, 2048, 512, 512
+FLOPS = 4 * 2 * R * N * D
+
+F32 = mybir.dt.float32
+BF16 = mybir.dt.bfloat16
+U32 = mybir.dt.uint32
+I32 = mybir.dt.int32
+U16 = mybir.dt.uint16
+U8 = mybir.dt.uint8
+E4M3 = mybir.dt.float8_e4m3fn_x4
+E5M2 = mybir.dt.float8_e5m2_x4
+ACT = mybir.ActivationFunctionType
+ALU = mybir.AluOpType
+
+P = 128
+PACK = 4
+CHUNK = 512
+Q_VECTOR = 88
+
+
+def tile_attend_gat_pl_sig_c_kernel(tc, qT, cT, doT, rw, qm, dom, offs, out_0, out_1, out_2):
+    nc = tc.nc
+    with ExitStack() as ctx:
+        keep = ctx.enter_context(tc.tile_pool(name="keep", bufs=1))
+        psum = ctx.enter_context(tc.psum_pool(name="psum", bufs=1))
+
+        def sb(name, shape, dtype):
+            return keep.tile(shape, dtype, name=name, align_bytes=64)
+
+        def flat(t):
+            return t[:].rearrange("p w j -> p (w j)")
+
+        offsets = keep.tile([P, N // 16], U16, name="offsets")
+        nc.sync.dma_start(offsets[:], offs)
+
+        pool_planes = [sb("pool%d" % j, [P, T], F32) for j in range(PACK)]
+        c_rows = cT.rearrange("(p j) t -> j p t", j=PACK)
+        for j in range(PACK):
+            nc.sync.dma_start(out=pool_planes[j][:], in_=c_rows[j])
+        raw = {}
+        gate = sb("gate", [P, PACK], F32)
+        for name, src in (("q", qT), ("do", doT), ("qm", qm), ("dom", dom)):
+            raw[name] = sb("raw_" + name, [P, PACK, 512], F32)
+            nc.sync.dma_start(out=raw[name][:], in_=src[0].rearrange("(p j) w -> p j w", j=PACK))
+            if name == "q":
+                nc.sync.dma_start(out=gate[:], in_=rw[0].rearrange("(p t) o -> p (t o)", t=PACK))
+
+        warm = sb("warm", [P, 8], F32)
+        warm_out = sb("warm_out", [P, 8], F32)
+        nc.vector.memset(warm[:], 0.0)
+        nc.scalar.activation(out=warm_out[:], in_=warm[:], func=ACT.Sigmoid)
+
+        windows = [sb("window%d" % j, [P, T], F32) for j in range(PACK)]
+        for j in range(PACK):
+            nc.vector.memset(windows[j][:], 0.0)
+
+        grouped = {name: sb("grouped_" + name, [P, 512, PACK], BF16) for name in ("c", "q", "do", "qm", "dom", "ds", "pw")}
+        codes = {name: sb("codes_" + name, [P, 512], U32) for name in grouped}
+        scales = {name: sb("scales_" + name, [P, 512], U8) for name in grouped}
+        fmt = {"c": E4M3, "q": E4M3, "do": E5M2, "qm": E4M3, "dom": E5M2, "ds": E5M2, "pw": E4M3}
+
+        def quantize(name, lo=0, hi=512):
+            nc.vector.quantize_mx(
+                out=codes[name][:, lo:hi].bitcast(fmt[name]),
+                scales=scales[name][:, lo:hi],
+                in_=flat(grouped[name])[:, PACK * lo : PACK * hi],
+            )
+
+        def deal(copy, name, m0=0, m1=P, t0=0, t1=PACK):
+            dst = grouped[name][:].rearrange("p (t m) j -> p m j t", t=PACK)
+            src = raw[name][:].rearrange("p j (m t) -> p m j t", t=PACK)
+            copy(out=dst[:, m0:m1, :, t0:t1], in_=src[:, m0:m1, :, t0:t1])
+
+        def mx(out, stat, tile_index, mov, start, stop):
+            cols = slice(P * tile_index, P * (tile_index + 1))
+            nc.tensor.matmul_mx(
+                out=out[:],
+                lhsT=codes[stat][:, cols].bitcast(fmt[stat]),
+                lhsT_scale=scales[stat][:, cols],
+                rhs=codes[mov][:].bitcast(fmt[mov]),
+                rhs_scale=scales[mov][:],
+                start=start,
+                stop=stop,
+            )
+
+        for j in range(PACK):
+            nc.vector.tensor_copy(out=grouped["c"][:, :, j], in_=pool_planes[j][:].indirect(offsets[:]))
+        quantize("c")
+        deal(nc.scalar.copy, "q", Q_VECTOR, P)
+        deal(nc.vector.tensor_copy, "q", 0, Q_VECTOR)
+        quantize("q")
+
+        score = [psum.tile([P, N], F32, name="score%d" % t, tag="bank%d" % t) for t in range(PACK)]
+        dprob = [psum.tile([P, N], F32, name="dprob%d" % t, tag="bank%d" % (PACK + t)) for t in range(PACK)]
+        for t in range(PACK):
+            mx(score[t], "q", t, "c", True, True)
+
+        prob = sb("prob", [P, PACK, N], F32)
+        for t in range(PACK):
+            nc.scalar.activation(out=prob[:, t, :], in_=score[t][:], func=ACT.Sigmoid)
+
+        deal(nc.vector.tensor_copy, "do")
+        quantize("do")
+        for t in range(PACK):
+            mx(dprob[t], "do", t, "c", True, True)
+
+        neg_pw = sb("neg_pw", [P, PACK, N], F32)
+        neg_dq = sb("neg_dq", [P, PACK, N], F32)
+        for t in range(PACK):
+            nc.vector.tensor_scalar(
+                out=neg_pw[:, t, :], in0=prob[:, t, :], scalar1=gate[:, t : t + 1], scalar2=-1.0,
+                op0=ALU.mult, op1=ALU.mult,
+            )
+            nc.vector.scalar_tensor_tensor(
+                out=neg_dq[:, t, :], in0=prob[:, t, :], scalar=1.0, in1=dprob[t][:],
+                op0=ALU.subtract, op1=ALU.mult,
+            )
+
+        def runs(t):
+            return t[:].rearrange("p t (c i) -> p c t i", i=4)
+
+        def woven(t):
+            return t[:].rearrange("p (c i) t -> p c t i", i=4)
+
+        deal(nc.scalar.copy, "qm", 0, P, 0, 2)
+        nc.scalar.activation(out=woven(grouped["pw"]), in_=runs(neg_pw), func=ACT.Copy, scale=-1.0)
+        deal(nc.scalar.copy, "dom", 0, P, 0, 2)
+        nc.vector.tensor_tensor(out=woven(grouped["ds"]), in0=runs(neg_dq), in1=runs(neg_pw), op=ALU.mult)
+        quantize("qm", 0, 256)
+        quantize("ds")
+        quantize("pw")
+        quantize("dom", 0, 256)
+        deal(nc.scalar.copy, "qm", 0, P, 2, 4)
+        deal(nc.scalar.copy, "dom", 0, P, 2, 4)
+
+        grad_sb = [sb("grad_sb%d" % j, [P, N], F32) for j in range(PACK)]
+        chunks = T // CHUNK
+        pairs = [sb("pairs%d" % c, [P, 2, CHUNK * 2], BF16) for c in range(chunks)]
+        out_rows = out_0.rearrange("(p j) t -> j p t", j=PACK)
+
+        def round_plane(copy, j, c):
+            dst = pairs[c][:, j // 2, :].rearrange("p (t e) -> p t e", e=2)
+            src = windows[j][:, CHUNK * c : CHUNK * (c + 1)]
+            if j == PACK - 2 and c < chunks // 2:
+                copy(out=dst, in_=src.unsqueeze(2).to_broadcast([P, CHUNK, 2]))
+            else:
+                copy(out=dst[:, :, j % 2], in_=src)
+
+        def product(j):
+            grad = psum.tile([P, N], F32, name="grad%d" % j, tag="bank%d" % j)
+            mx(grad, "qm", j, "ds", True, False)
+            mx(grad, "dom", j, "pw", False, True)
+            nc.scalar.copy(out=grad_sb[j][:], in_=grad[:])
+
+        product(0)
+        product(1)
+        quantize("qm", 256, 512)
+        quantize("dom", 256, 512)
+        product(2)
+        product(3)
+        for j in range(PACK):
+            nc.vector.tensor_copy(out=windows[j][:].indirect(offsets[:]), in_=grad_sb[j][:])
+            nc.sync.dma_start(out=out_rows[j], in_=windows[j][:])
+            if j < PACK - 1:
+                for c in range(chunks):
+                    round_plane(nc.scalar.copy, j, c)
+
+        out_grouped = [sb("out_grouped%d" % c, [P, CHUNK * PACK], BF16) for c in range(chunks)]
+        out_codes = sb("out_codes", [P, T], U32)
+        out_scales = sb("out_scales", [P, T], U8)
+        words_dram = out_1[0].rearrange("p t l -> p (t l)").bitcast(I32)
+        copies = [nc.vector.tensor_copy if c < chunks // 2 else nc.scalar.copy for c in range(chunks)]
+
+        def finish_pairs(c):
+            round_plane(copies[c], PACK - 1, c)
+
+        def weave(c):
+            src = pairs[c][:].bitcast(F32).rearrange("p u (c i) -> p c u i", i=4)
+            dst = out_grouped[c][:].bitcast(F32).rearrange("p (c i u) -> p c u i", i=4, u=2)
+            copies[c](out=dst, in_=src)
+
+        finish_pairs(0)
+        finish_pairs(1)
+        weave(0)
+        weave(1)
+        for c in (2, 3):
+            finish_pairs(c)
+            weave(c)
+        for c in range(chunks):
+            lo, hi = CHUNK * c, CHUNK * (c + 1)
+            nc.vector.quantize_mx(
+                out=out_codes[:, lo:hi].bitcast(E4M3),
+                scales=out_scales[:, lo:hi],
+                in_=out_grouped[c][:],
+            )
+            nc.sync.dma_start(out=words_dram[:, lo:hi], in_=out_codes[:, lo:hi].bitcast(I32))
+        for quad in range(4):
+            nc.sync.dma_start(
+                out=out_2[0, 4 * quad : 4 * quad + 4, :].bitcast(I32),
+                in_=out_scales[32 * quad : 32 * quad + 4, :].bitcast(I32),
+            )

@@ -18,8 +18,9 @@ ALU = mybir.AluOpType
 
 P = 128
 PACK = 4
-CHUNK = 512
-Q_VECTOR = 88
+DO_VECTOR = 80
+VECTOR_CHUNKS = ((0, 512), (512, 896))
+SCALAR_CHUNKS = ((896, 1408), (1408, 1920), (1920, 2048))
 
 
 def tile_attend_gat_pl_sig_c_kernel(tc, qT, cT, doT, rw, qm, dom, offs, out_0, out_1, out_2):
@@ -28,8 +29,8 @@ def tile_attend_gat_pl_sig_c_kernel(tc, qT, cT, doT, rw, qm, dom, offs, out_0, o
         keep = ctx.enter_context(tc.tile_pool(name="keep", bufs=1))
         psum = ctx.enter_context(tc.psum_pool(name="psum", bufs=1))
 
-        def sb(name, shape, dtype):
-            return keep.tile(shape, dtype, name=name, align_bytes=64)
+        def sb(name, shape, dtype, tag=None):
+            return keep.tile(shape, dtype, name=name, tag=tag or name, align_bytes=64)
 
         def flat(t):
             return t[:].rearrange("p w j -> p (w j)")
@@ -39,15 +40,19 @@ def tile_attend_gat_pl_sig_c_kernel(tc, qT, cT, doT, rw, qm, dom, offs, out_0, o
 
         pool_planes = [sb("pool%d" % j, [P, T], F32) for j in range(PACK)]
         c_rows = cT.rearrange("(p j) t -> j p t", j=PACK)
+        raw = {name: sb("raw_" + name, [P, PACK, 512], F32) for name in ("q", "do", "qm", "dom")}
+        gate = sb("gate", [P, PACK], F32)
+
+        def load(name, src):
+            nc.sync.dma_start(out=raw[name][:], in_=src[0].rearrange("(p j) w -> p j w", j=PACK))
+
+        load("q", qT)
         for j in range(PACK):
             nc.sync.dma_start(out=pool_planes[j][:], in_=c_rows[j])
-        raw = {}
-        gate = sb("gate", [P, PACK], F32)
-        for name, src in (("q", qT), ("do", doT), ("qm", qm), ("dom", dom)):
-            raw[name] = sb("raw_" + name, [P, PACK, 512], F32)
-            nc.sync.dma_start(out=raw[name][:], in_=src[0].rearrange("(p j) w -> p j w", j=PACK))
-            if name == "q":
-                nc.sync.dma_start(out=gate[:], in_=rw[0].rearrange("(p t) o -> p (t o)", t=PACK))
+        load("do", doT)
+        nc.sync.dma_start(out=gate[:], in_=rw[0].rearrange("(p t) o -> p (t o)", t=PACK))
+        load("qm", qm)
+        load("dom", dom)
 
         warm = sb("warm", [P, 8], F32)
         warm_out = sb("warm_out", [P, 8], F32)
@@ -87,34 +92,37 @@ def tile_attend_gat_pl_sig_c_kernel(tc, qT, cT, doT, rw, qm, dom, offs, out_0, o
                 stop=stop,
             )
 
+        deal(nc.scalar.copy, "q")
         for j in range(PACK):
+            if j == PACK - 1:
+                quantize("q")
             nc.vector.tensor_copy(out=grouped["c"][:, :, j], in_=pool_planes[j][:].indirect(offsets[:]))
         quantize("c")
-        deal(nc.scalar.copy, "q", Q_VECTOR, P)
-        deal(nc.vector.tensor_copy, "q", 0, Q_VECTOR)
-        quantize("q")
+        deal(nc.scalar.copy, "do", DO_VECTOR, P)
+        deal(nc.vector.tensor_copy, "do", 0, DO_VECTOR)
 
         score = [psum.tile([P, N], F32, name="score%d" % t, tag="bank%d" % t) for t in range(PACK)]
         dprob = [psum.tile([P, N], F32, name="dprob%d" % t, tag="bank%d" % (PACK + t)) for t in range(PACK)]
         for t in range(PACK):
             mx(score[t], "q", t, "c", True, True)
 
-        prob = sb("prob", [P, PACK, N], F32)
+        prob = sb("prob", [P, PACK, N], F32, "raw_do")
         for t in range(PACK):
             nc.scalar.activation(out=prob[:, t, :], in_=score[t][:], func=ACT.Sigmoid)
 
-        deal(nc.vector.tensor_copy, "do")
-        quantize("do")
+        quantize("do", 0, 256)
+        quantize("do", 256, 512)
         for t in range(PACK):
             mx(dprob[t], "do", t, "c", True, True)
 
         neg_pw = sb("neg_pw", [P, PACK, N], F32)
         neg_dq = sb("neg_dq", [P, PACK, N], F32)
         for t in range(PACK):
-            nc.vector.tensor_scalar(
+            nc.gpsimd.tensor_scalar(
                 out=neg_pw[:, t, :], in0=prob[:, t, :], scalar1=gate[:, t : t + 1], scalar2=-1.0,
                 op0=ALU.mult, op1=ALU.mult,
             )
+        for t in range(PACK):
             nc.vector.scalar_tensor_tensor(
                 out=neg_dq[:, t, :], in0=prob[:, t, :], scalar=1.0, in1=dprob[t][:],
                 op0=ALU.subtract, op1=ALU.mult,
@@ -138,22 +146,19 @@ def tile_attend_gat_pl_sig_c_kernel(tc, qT, cT, doT, rw, qm, dom, offs, out_0, o
         deal(nc.scalar.copy, "dom", 0, P, 2, 4)
 
         grad_sb = [sb("grad_sb%d" % j, [P, N], F32) for j in range(PACK)]
-        chunks = T // CHUNK
-        pairs = [sb("pairs%d" % c, [P, 2, CHUNK * 2], BF16) for c in range(chunks)]
+        chunks = VECTOR_CHUNKS + SCALAR_CHUNKS
         out_rows = out_0.rearrange("(p j) t -> j p t", j=PACK)
 
         def round_plane(copy, j, c):
-            dst = pairs[c][:, j // 2, :].rearrange("p (t e) -> p t e", e=2)
-            src = windows[j][:, CHUNK * c : CHUNK * (c + 1)]
-            if j == PACK - 2 and c < chunks // 2:
-                copy(out=dst, in_=src.unsqueeze(2).to_broadcast([P, CHUNK, 2]))
-            else:
-                copy(out=dst[:, :, j % 2], in_=src)
+            dst = pair_view(c)[:, j // 2, :].rearrange("p (t e) -> p t e", e=2)
+            copy(out=dst[:, :, j % 2], in_=windows[j][:, c[0] : c[1]])
 
         def product(j):
             grad = psum.tile([P, N], F32, name="grad%d" % j, tag="bank%d" % j)
-            mx(grad, "qm", j, "ds", True, False)
-            mx(grad, "dom", j, "pw", False, True)
+            passes = (("qm", "ds"), ("dom", "pw"))
+            first, last = passes if j == 0 else passes[::-1]
+            mx(grad, first[0], j, first[1], True, False)
+            mx(grad, last[0], j, last[1], False, True)
             nc.scalar.copy(out=grad_sb[j][:], in_=grad[:])
 
         product(0)
@@ -162,44 +167,63 @@ def tile_attend_gat_pl_sig_c_kernel(tc, qT, cT, doT, rw, qm, dom, offs, out_0, o
         quantize("dom", 256, 512)
         product(2)
         product(3)
+        spans = ((0, VECTOR_CHUNKS[-1][1]),) + SCALAR_CHUNKS
+        freed = ("codes_ds", "codes_qm", "scales_ds", "scales_qm")
+        pairs = {s: sb("pairs%d" % s[0], [P, 2, (s[1] - s[0]) * 2], BF16, tag) for s, tag in zip(spans, freed)}
+
+        def pair_view(c):
+            s = c if c in pairs else spans[0]
+            return pairs[s][:, :, 2 * (c[0] - s[0]) : 2 * (c[1] - s[0])]
+
         for j in range(PACK):
             nc.vector.tensor_copy(out=windows[j][:].indirect(offsets[:]), in_=grad_sb[j][:])
             nc.sync.dma_start(out=out_rows[j], in_=windows[j][:])
             if j < PACK - 1:
-                for c in range(chunks):
+                for c in spans if j < 2 else SCALAR_CHUNKS:
                     round_plane(nc.scalar.copy, j, c)
 
-        out_grouped = [sb("out_grouped%d" % c, [P, CHUNK * PACK], BF16) for c in range(chunks)]
+        out_grouped = {c: sb("out_grouped%d" % c[0], [P, (c[1] - c[0]) * PACK], BF16) for c in chunks}
         out_codes = sb("out_codes", [P, T], U32)
         out_scales = sb("out_scales", [P, T], U8)
         words_dram = out_1[0].rearrange("p t l -> p (t l)").bitcast(I32)
-        copies = [nc.vector.tensor_copy if c < chunks // 2 else nc.scalar.copy for c in range(chunks)]
 
-        def finish_pairs(c):
-            round_plane(copies[c], PACK - 1, c)
-
-        def weave(c):
-            src = pairs[c][:].bitcast(F32).rearrange("p u (c i) -> p c u i", i=4)
+        def weave(copy, c):
+            src = pair_view(c).bitcast(F32).rearrange("p u (c i) -> p c u i", i=4)
             dst = out_grouped[c][:].bitcast(F32).rearrange("p (c i u) -> p c u i", i=4, u=2)
-            copies[c](out=dst, in_=src)
+            copy(out=dst, in_=src)
 
-        finish_pairs(0)
-        finish_pairs(1)
-        weave(0)
-        weave(1)
-        for c in (2, 3):
-            finish_pairs(c)
-            weave(c)
-        for c in range(chunks):
-            lo, hi = CHUNK * c, CHUNK * (c + 1)
-            nc.vector.quantize_mx(
-                out=out_codes[:, lo:hi].bitcast(E4M3),
-                scales=out_scales[:, lo:hi],
-                in_=out_grouped[c][:],
-            )
+        def quantize_out(c):
+            lo = c[0]
+            for width in (512, 256, 128):
+                if c[1] - lo >= width:
+                    nc.vector.quantize_mx(
+                        out=out_codes[:, lo : lo + width].bitcast(E4M3),
+                        scales=out_scales[:, lo : lo + width],
+                        in_=out_grouped[c][:, PACK * (lo - c[0]) : PACK * (lo - c[0] + width)],
+                    )
+                    lo = lo + width
+
+        def store_words(lo, hi):
             nc.sync.dma_start(out=words_dram[:, lo:hi], in_=out_codes[:, lo:hi].bitcast(I32))
+
+        round_plane(nc.vector.tensor_copy, 2, spans[0])
+        round_plane(nc.vector.tensor_copy, 3, spans[0])
+        for c in VECTOR_CHUNKS:
+            weave(nc.vector.tensor_copy, c)
+        for c in SCALAR_CHUNKS:
+            round_plane(nc.scalar.copy, 3, c)
+            weave(nc.scalar.copy, c)
+        quantize_out(chunks[0])
+        quantize_out(chunks[1])
+        store_words(0, 896)
+        quantize_out(chunks[2])
+        store_words(896, 1408)
+        quantize_out(chunks[3])
+        store_words(1408, 1920)
+        quantize_out(chunks[4])
+        store_words(1920, 2048)
         for quad in range(4):
-            nc.sync.dma_start(
+            nc.scalar.dma_start(
                 out=out_2[0, 4 * quad : 4 * quad + 4, :].bitcast(I32),
                 in_=out_scales[32 * quad : 32 * quad + 4, :].bitcast(I32),
             )

@@ -18,9 +18,8 @@ ALU = mybir.AluOpType
 
 P = 128
 PACK = 4
-DO_VECTOR = 80
-VECTOR_CHUNKS = ((0, 512), (512, 896))
-SCALAR_CHUNKS = ((896, 1408), (1408, 1920), (1920, 2048))
+VECTOR_CHUNKS = ((0, 512), (512, 1024))
+SCALAR_CHUNKS = ((1024, 1536), (1536, 1920), (1920, 2048))
 
 
 def tile_attend_gat_pl_sig_c_kernel(tc, qT, cT, doT, rw, qm, dom, offs, out_0, out_1, out_2):
@@ -46,11 +45,11 @@ def tile_attend_gat_pl_sig_c_kernel(tc, qT, cT, doT, rw, qm, dom, offs, out_0, o
         def load(name, src):
             nc.sync.dma_start(out=raw[name][:], in_=src[0].rearrange("(p j) w -> p j w", j=PACK))
 
-        load("q", qT)
         for j in range(PACK):
             nc.sync.dma_start(out=pool_planes[j][:], in_=c_rows[j])
-        load("do", doT)
         nc.sync.dma_start(out=gate[:], in_=rw[0].rearrange("(p t) o -> p (t o)", t=PACK))
+        load("q", qT)
+        load("do", doT)
         load("qm", qm)
         load("dom", dom)
 
@@ -61,24 +60,29 @@ def tile_attend_gat_pl_sig_c_kernel(tc, qT, cT, doT, rw, qm, dom, offs, out_0, o
 
         windows = [sb("window%d" % j, [P, T], F32) for j in range(PACK)]
         for j in range(PACK):
-            nc.vector.memset(windows[j][:], 0.0)
+            (nc.vector if j < 2 else nc.gpsimd).memset(windows[j][:], 0.0)
 
-        grouped = {name: sb("grouped_" + name, [P, 512, PACK], BF16) for name in ("c", "q", "do", "qm", "dom", "ds", "pw")}
-        codes = {name: sb("codes_" + name, [P, 512], U32) for name in grouped}
-        scales = {name: sb("scales_" + name, [P, 512], U8) for name in grouped}
+        grouped = {name: sb("grouped_" + name, [P, 512, PACK], BF16) for name in ("c", "ds", "pw")}
+        names = ("c", "q", "do", "qm", "dom", "ds", "pw")
+        codes = {name: sb("codes_" + name, [P, 512], U32) for name in names}
+        scales = {name: sb("scales_" + name, [P, 512], U8) for name in names}
+        dealt = {}
         fmt = {"c": E4M3, "q": E4M3, "do": E5M2, "qm": E4M3, "dom": E5M2, "ds": E5M2, "pw": E4M3}
 
-        def quantize(name, lo=0, hi=512):
-            nc.vector.quantize_mx(
-                out=codes[name][:, lo:hi].bitcast(fmt[name]),
-                scales=scales[name][:, lo:hi],
-                in_=flat(grouped[name])[:, PACK * lo : PACK * hi],
-            )
+        def quantize(name):
+            nc.vector.quantize_mx(out=codes[name][:].bitcast(fmt[name]), scales=scales[name][:], in_=flat(grouped[name]))
 
-        def deal(copy, name, m0=0, m1=P, t0=0, t1=PACK):
-            dst = grouped[name][:].rearrange("p (t m) j -> p m j t", t=PACK)
+        def deal(copy, name, half, tag):
+            dealt[name, half] = sb("dealt_%s%d" % (name, half), [P, 2 * P, PACK], BF16, tag)
+            dst = dealt[name, half][:].rearrange("p (t m) j -> p m j t", t=2)
             src = raw[name][:].rearrange("p j (m t) -> p m j t", t=PACK)
-            copy(out=dst[:, m0:m1, :, t0:t1], in_=src[:, m0:m1, :, t0:t1])
+            copy(out=dst, in_=src[:, :, :, 2 * half : 2 * half + 2])
+
+        def quantize_dealt(name, half):
+            cols = slice(2 * P * half, 2 * P * (half + 1))
+            nc.vector.quantize_mx(
+                out=codes[name][:, cols].bitcast(fmt[name]), scales=scales[name][:, cols], in_=flat(dealt[name, half])
+            )
 
         def mx(out, stat, tile_index, mov, start, stop):
             cols = slice(P * tile_index, P * (tile_index + 1))
@@ -92,39 +96,40 @@ def tile_attend_gat_pl_sig_c_kernel(tc, qT, cT, doT, rw, qm, dom, offs, out_0, o
                 stop=stop,
             )
 
-        deal(nc.scalar.copy, "q")
         for j in range(PACK):
-            if j == PACK - 1:
-                quantize("q")
             nc.vector.tensor_copy(out=grouped["c"][:, :, j], in_=pool_planes[j][:].indirect(offsets[:]))
         quantize("c")
-        deal(nc.scalar.copy, "do", DO_VECTOR, P)
-        deal(nc.vector.tensor_copy, "do", 0, DO_VECTOR)
+        deal(nc.scalar.copy, "q", 1, "dealt_high")
+        deal(nc.vector.tensor_copy, "q", 0, "dealt_low")
+        quantize_dealt("q", 0)
+        quantize_dealt("q", 1)
+        deal(nc.scalar.copy, "do", 1, "dealt_high")
+        deal(nc.vector.tensor_copy, "do", 0, "dealt_low")
 
         score = [psum.tile([P, N], F32, name="score%d" % t, tag="bank%d" % t) for t in range(PACK)]
         dprob = [psum.tile([P, N], F32, name="dprob%d" % t, tag="bank%d" % (PACK + t)) for t in range(PACK)]
         for t in range(PACK):
             mx(score[t], "q", t, "c", True, True)
 
-        prob = sb("prob", [P, PACK, N], F32, "raw_do")
+        prob = [sb("prob%d" % t, [P, N], F32) for t in range(PACK)]
         for t in range(PACK):
-            nc.scalar.activation(out=prob[:, t, :], in_=score[t][:], func=ACT.Sigmoid)
+            nc.scalar.activation(out=prob[t][:], in_=score[t][:], func=ACT.Sigmoid)
 
-        quantize("do", 0, 256)
-        quantize("do", 256, 512)
+        quantize_dealt("do", 0)
+        quantize_dealt("do", 1)
         for t in range(PACK):
             mx(dprob[t], "do", t, "c", True, True)
 
         neg_pw = sb("neg_pw", [P, PACK, N], F32)
         neg_dq = sb("neg_dq", [P, PACK, N], F32)
         for t in range(PACK):
-            nc.gpsimd.tensor_scalar(
-                out=neg_pw[:, t, :], in0=prob[:, t, :], scalar1=gate[:, t : t + 1], scalar2=-1.0,
+            nc.vector.tensor_scalar(
+                out=neg_pw[:, t, :], in0=prob[t][:], scalar1=gate[:, t : t + 1], scalar2=-1.0,
                 op0=ALU.mult, op1=ALU.mult,
             )
         for t in range(PACK):
             nc.vector.scalar_tensor_tensor(
-                out=neg_dq[:, t, :], in0=prob[:, t, :], scalar=1.0, in1=dprob[t][:],
+                out=neg_dq[:, t, :], in0=prob[t][:], scalar=1.0, in1=dprob[t][:],
                 op0=ALU.subtract, op1=ALU.mult,
             )
 
@@ -134,16 +139,16 @@ def tile_attend_gat_pl_sig_c_kernel(tc, qT, cT, doT, rw, qm, dom, offs, out_0, o
         def woven(t):
             return t[:].rearrange("p (c i) t -> p c t i", i=4)
 
-        deal(nc.scalar.copy, "qm", 0, P, 0, 2)
+        deal(nc.scalar.copy, "qm", 0, "dealt_high")
         nc.scalar.activation(out=woven(grouped["pw"]), in_=runs(neg_pw), func=ACT.Copy, scale=-1.0)
-        deal(nc.scalar.copy, "dom", 0, P, 0, 2)
+        deal(nc.scalar.copy, "dom", 0, "prob2")
+        quantize_dealt("qm", 0)
         nc.vector.tensor_tensor(out=woven(grouped["ds"]), in0=runs(neg_dq), in1=runs(neg_pw), op=ALU.mult)
-        quantize("qm", 0, 256)
-        quantize("ds")
         quantize("pw")
-        quantize("dom", 0, 256)
-        deal(nc.scalar.copy, "qm", 0, P, 2, 4)
-        deal(nc.scalar.copy, "dom", 0, P, 2, 4)
+        quantize_dealt("dom", 0)
+        quantize("ds")
+        deal(nc.scalar.copy, "qm", 1, "prob3")
+        deal(nc.scalar.copy, "dom", 1, "neg_dq")
 
         grad_sb = [sb("grad_sb%d" % j, [P, N], F32) for j in range(PACK)]
         chunks = VECTOR_CHUNKS + SCALAR_CHUNKS
@@ -151,24 +156,31 @@ def tile_attend_gat_pl_sig_c_kernel(tc, qT, cT, doT, rw, qm, dom, offs, out_0, o
 
         def round_plane(copy, j, c):
             dst = pair_view(c)[:, j // 2, :].rearrange("p (t e) -> p t e", e=2)
-            copy(out=dst[:, :, j % 2], in_=windows[j][:, c[0] : c[1]])
+            src = windows[j][:, c[0] : c[1]]
+            if j == 2 and c == spans[0]:
+                copy(out=dst, in_=src.unsqueeze(2).to_broadcast([P, c[1] - c[0], 2]))
+            else:
+                copy(out=dst[:, :, j % 2], in_=src)
+
+        pieces = [((0, N // 2), (N // 2, N))] + [((0, N),)] * (PACK - 1)
 
         def product(j):
             grad = psum.tile([P, N], F32, name="grad%d" % j, tag="bank%d" % j)
-            passes = (("qm", "ds"), ("dom", "pw"))
+            passes = (("dom", "pw"), ("qm", "ds"))
             first, last = passes if j == 0 else passes[::-1]
             mx(grad, first[0], j, first[1], True, False)
             mx(grad, last[0], j, last[1], False, True)
-            nc.scalar.copy(out=grad_sb[j][:], in_=grad[:])
+            for lo, hi in pieces[j]:
+                nc.scalar.copy(out=grad_sb[j][:, lo:hi], in_=grad[:, lo:hi])
 
         product(0)
         product(1)
-        quantize("qm", 256, 512)
-        quantize("dom", 256, 512)
+        quantize_dealt("qm", 1)
+        quantize_dealt("dom", 1)
         product(2)
         product(3)
         spans = ((0, VECTOR_CHUNKS[-1][1]),) + SCALAR_CHUNKS
-        freed = ("codes_ds", "codes_qm", "scales_ds", "scales_qm")
+        freed = ("codes_pw", "codes_dom", "scales_pw", "scales_dom")
         pairs = {s: sb("pairs%d" % s[0], [P, 2, (s[1] - s[0]) * 2], BF16, tag) for s, tag in zip(spans, freed)}
 
         def pair_view(c):
@@ -176,10 +188,13 @@ def tile_attend_gat_pl_sig_c_kernel(tc, qT, cT, doT, rw, qm, dom, offs, out_0, o
             return pairs[s][:, :, 2 * (c[0] - s[0]) : 2 * (c[1] - s[0])]
 
         for j in range(PACK):
-            nc.vector.tensor_copy(out=windows[j][:].indirect(offsets[:]), in_=grad_sb[j][:])
+            for lo, hi in pieces[j]:
+                nc.vector.tensor_copy(
+                    out=windows[j][:].indirect(offsets[:, lo // 16 : hi // 16]), in_=grad_sb[j][:, lo:hi]
+                )
             nc.sync.dma_start(out=out_rows[j], in_=windows[j][:])
             if j < PACK - 1:
-                for c in spans if j < 2 else SCALAR_CHUNKS:
+                for c in spans:
                     round_plane(nc.scalar.copy, j, c)
 
         out_grouped = {c: sb("out_grouped%d" % c[0], [P, (c[1] - c[0]) * PACK], BF16) for c in chunks}
@@ -206,22 +221,19 @@ def tile_attend_gat_pl_sig_c_kernel(tc, qT, cT, doT, rw, qm, dom, offs, out_0, o
         def store_words(lo, hi):
             nc.sync.dma_start(out=words_dram[:, lo:hi], in_=out_codes[:, lo:hi].bitcast(I32))
 
-        round_plane(nc.vector.tensor_copy, 2, spans[0])
-        round_plane(nc.vector.tensor_copy, 3, spans[0])
+        for c in VECTOR_CHUNKS:
+            round_plane(nc.vector.tensor_copy, 3, c)
         for c in VECTOR_CHUNKS:
             weave(nc.vector.tensor_copy, c)
         for c in SCALAR_CHUNKS:
             round_plane(nc.scalar.copy, 3, c)
             weave(nc.scalar.copy, c)
-        quantize_out(chunks[0])
-        quantize_out(chunks[1])
-        store_words(0, 896)
-        quantize_out(chunks[2])
-        store_words(896, 1408)
-        quantize_out(chunks[3])
-        store_words(1408, 1920)
-        quantize_out(chunks[4])
-        store_words(1920, 2048)
+        for c in VECTOR_CHUNKS:
+            quantize_out(c)
+        store_words(spans[0][0], spans[0][1])
+        for c in SCALAR_CHUNKS:
+            quantize_out(c)
+            store_words(c[0], c[1])
         for quad in range(4):
             nc.scalar.dma_start(
                 out=out_2[0, 4 * quad : 4 * quad + 4, :].bitcast(I32),

@@ -18,8 +18,8 @@ ALU = mybir.AluOpType
 
 P = 128
 PACK = 4
-VECTOR_CHUNKS = ((0, 512), (512, 1024))
-SCALAR_CHUNKS = ((1024, 1536), (1536, 1920), (1920, 2048))
+VECTOR_CHUNKS = ((0, 512), (512, 1152))
+SCALAR_CHUNKS = ((1152, 1664), (1664, 1920), (1920, 2048))
 
 
 def tile_attend_gat_pl_sig_c_kernel(tc, qT, cT, doT, rw, qm, dom, offs, out_0, out_1, out_2):
@@ -47,20 +47,15 @@ def tile_attend_gat_pl_sig_c_kernel(tc, qT, cT, doT, rw, qm, dom, offs, out_0, o
 
         for j in range(PACK):
             nc.sync.dma_start(out=pool_planes[j][:], in_=c_rows[j])
-        nc.sync.dma_start(out=gate[:], in_=rw[0].rearrange("(p t) o -> p (t o)", t=PACK))
         load("q", qT)
         load("do", doT)
+        nc.sync.dma_start(out=gate[:], in_=rw[0].rearrange("(p t) o -> p (t o)", t=PACK))
         load("qm", qm)
         load("dom", dom)
 
-        warm = sb("warm", [P, 8], F32)
-        warm_out = sb("warm_out", [P, 8], F32)
-        nc.vector.memset(warm[:], 0.0)
-        nc.scalar.activation(out=warm_out[:], in_=warm[:], func=ACT.Sigmoid)
-
         windows = [sb("window%d" % j, [P, T], F32) for j in range(PACK)]
         for j in range(PACK):
-            (nc.vector if j < 2 else nc.gpsimd).memset(windows[j][:], 0.0)
+            nc.vector.memset(windows[j][:], 0.0)
 
         grouped = {name: sb("grouped_" + name, [P, 512, PACK], BF16) for name in ("c", "ds", "pw")}
         names = ("c", "q", "do", "qm", "dom", "ds", "pw")
@@ -78,10 +73,13 @@ def tile_attend_gat_pl_sig_c_kernel(tc, qT, cT, doT, rw, qm, dom, offs, out_0, o
             src = raw[name][:].rearrange("p j (m t) -> p m j t", t=PACK)
             copy(out=dst, in_=src[:, :, :, 2 * half : 2 * half + 2])
 
-        def quantize_dealt(name, half):
-            cols = slice(2 * P * half, 2 * P * (half + 1))
+        def quantize_dealt(name, first, count):
+            cols = slice(P * first, P * (first + count))
+            lo = PACK * P * (first % 2)
             nc.vector.quantize_mx(
-                out=codes[name][:, cols].bitcast(fmt[name]), scales=scales[name][:, cols], in_=flat(dealt[name, half])
+                out=codes[name][:, cols].bitcast(fmt[name]),
+                scales=scales[name][:, cols],
+                in_=flat(dealt[name, first // 2])[:, lo : lo + PACK * P * count],
             )
 
         def mx(out, stat, tile_index, mov, start, stop):
@@ -99,12 +97,12 @@ def tile_attend_gat_pl_sig_c_kernel(tc, qT, cT, doT, rw, qm, dom, offs, out_0, o
         for j in range(PACK):
             nc.vector.tensor_copy(out=grouped["c"][:, :, j], in_=pool_planes[j][:].indirect(offsets[:]))
         quantize("c")
-        deal(nc.scalar.copy, "q", 1, "dealt_high")
         deal(nc.vector.tensor_copy, "q", 0, "dealt_low")
-        quantize_dealt("q", 0)
-        quantize_dealt("q", 1)
-        deal(nc.scalar.copy, "do", 1, "dealt_high")
+        deal(nc.vector.tensor_copy, "q", 1, "dealt_high")
+        quantize_dealt("q", 0, 2)
+        quantize_dealt("q", 2, 2)
         deal(nc.vector.tensor_copy, "do", 0, "dealt_low")
+        deal(nc.vector.tensor_copy, "do", 1, "dealt_high")
 
         score = [psum.tile([P, N], F32, name="score%d" % t, tag="bank%d" % t) for t in range(PACK)]
         dprob = [psum.tile([P, N], F32, name="dprob%d" % t, tag="bank%d" % (PACK + t)) for t in range(PACK)]
@@ -115,8 +113,8 @@ def tile_attend_gat_pl_sig_c_kernel(tc, qT, cT, doT, rw, qm, dom, offs, out_0, o
         for t in range(PACK):
             nc.scalar.activation(out=prob[t][:], in_=score[t][:], func=ACT.Sigmoid)
 
-        quantize_dealt("do", 0)
-        quantize_dealt("do", 1)
+        quantize_dealt("do", 0, 2)
+        quantize_dealt("do", 2, 2)
         for t in range(PACK):
             mx(dprob[t], "do", t, "c", True, True)
 
@@ -134,21 +132,25 @@ def tile_attend_gat_pl_sig_c_kernel(tc, qT, cT, doT, rw, qm, dom, offs, out_0, o
             )
 
         def runs(t):
-            return t[:].rearrange("p t (c i) -> p c t i", i=4)
+            return t[:].rearrange("p t (c i) -> p c t i", i=2)
 
         def woven(t):
-            return t[:].rearrange("p (c i) t -> p c t i", i=4)
+            return t[:].rearrange("p (c i) t -> p c t i", i=2)
 
         deal(nc.scalar.copy, "qm", 0, "dealt_high")
         nc.scalar.activation(out=woven(grouped["pw"]), in_=runs(neg_pw), func=ACT.Copy, scale=-1.0)
         deal(nc.scalar.copy, "dom", 0, "prob2")
-        quantize_dealt("qm", 0)
+        quantize_dealt("qm", 0, 1)
         nc.vector.tensor_tensor(out=woven(grouped["ds"]), in0=runs(neg_dq), in1=runs(neg_pw), op=ALU.mult)
         quantize("pw")
-        quantize_dealt("dom", 0)
+        quantize_dealt("dom", 0, 1)
         quantize("ds")
         deal(nc.scalar.copy, "qm", 1, "prob3")
         deal(nc.scalar.copy, "dom", 1, "neg_dq")
+        quantize_dealt("qm", 1, 1)
+        quantize_dealt("dom", 1, 1)
+        quantize_dealt("qm", 2, 2)
+        quantize_dealt("dom", 2, 2)
 
         grad_sb = [sb("grad_sb%d" % j, [P, N], F32) for j in range(PACK)]
         chunks = VECTOR_CHUNKS + SCALAR_CHUNKS
@@ -162,36 +164,26 @@ def tile_attend_gat_pl_sig_c_kernel(tc, qT, cT, doT, rw, qm, dom, offs, out_0, o
             else:
                 copy(out=dst[:, :, j % 2], in_=src)
 
-        pieces = [((0, N // 2), (N // 2, N))] + [((0, N),)] * (PACK - 1)
-
         def product(j):
             grad = psum.tile([P, N], F32, name="grad%d" % j, tag="bank%d" % j)
             passes = (("dom", "pw"), ("qm", "ds"))
             first, last = passes if j == 0 else passes[::-1]
             mx(grad, first[0], j, first[1], True, False)
             mx(grad, last[0], j, last[1], False, True)
-            for lo, hi in pieces[j]:
-                nc.scalar.copy(out=grad_sb[j][:, lo:hi], in_=grad[:, lo:hi])
+            nc.scalar.copy(out=grad_sb[j][:], in_=grad[:])
 
-        product(0)
-        product(1)
-        quantize_dealt("qm", 1)
-        quantize_dealt("dom", 1)
-        product(2)
-        product(3)
-        spans = ((0, VECTOR_CHUNKS[-1][1]),) + SCALAR_CHUNKS
-        freed = ("codes_pw", "codes_dom", "scales_pw", "scales_dom")
+        for j in range(PACK):
+            product(j)
+        spans = ((0, VECTOR_CHUNKS[-1][1]), (SCALAR_CHUNKS[0][0], T))
+        freed = ("codes_pw", "codes_dom")
         pairs = {s: sb("pairs%d" % s[0], [P, 2, (s[1] - s[0]) * 2], BF16, tag) for s, tag in zip(spans, freed)}
 
         def pair_view(c):
-            s = c if c in pairs else spans[0]
+            s = spans[0] if c[0] < spans[0][1] else spans[1]
             return pairs[s][:, :, 2 * (c[0] - s[0]) : 2 * (c[1] - s[0])]
 
         for j in range(PACK):
-            for lo, hi in pieces[j]:
-                nc.vector.tensor_copy(
-                    out=windows[j][:].indirect(offsets[:, lo // 16 : hi // 16]), in_=grad_sb[j][:, lo:hi]
-                )
+            nc.vector.tensor_copy(out=windows[j][:].indirect(offsets[:]), in_=grad_sb[j][:])
             nc.sync.dma_start(out=out_rows[j], in_=windows[j][:])
             if j < PACK - 1:
                 for c in spans:
@@ -203,8 +195,8 @@ def tile_attend_gat_pl_sig_c_kernel(tc, qT, cT, doT, rw, qm, dom, offs, out_0, o
         words_dram = out_1[0].rearrange("p t l -> p (t l)").bitcast(I32)
 
         def weave(copy, c):
-            src = pair_view(c).bitcast(F32).rearrange("p u (c i) -> p c u i", i=4)
-            dst = out_grouped[c][:].bitcast(F32).rearrange("p (c i u) -> p c u i", i=4, u=2)
+            src = pair_view(c).bitcast(F32).rearrange("p u t -> p t u")
+            dst = out_grouped[c][:].bitcast(F32).rearrange("p (t u) -> p t u", u=2)
             copy(out=dst, in_=src)
 
         def quantize_out(c):
@@ -225,16 +217,16 @@ def tile_attend_gat_pl_sig_c_kernel(tc, qT, cT, doT, rw, qm, dom, offs, out_0, o
             round_plane(nc.vector.tensor_copy, 3, c)
         for c in VECTOR_CHUNKS:
             weave(nc.vector.tensor_copy, c)
+        round_plane(nc.scalar.copy, 3, spans[1])
         for c in SCALAR_CHUNKS:
-            round_plane(nc.scalar.copy, 3, c)
             weave(nc.scalar.copy, c)
-        for c in VECTOR_CHUNKS:
-            quantize_out(c)
-        store_words(spans[0][0], spans[0][1])
-        for c in SCALAR_CHUNKS:
+        for c in chunks[:3]:
             quantize_out(c)
             store_words(c[0], c[1])
-        for quad in range(4):
+        for c in chunks[3:]:
+            quantize_out(c)
+        store_words(chunks[3][0], T)
+        for quad in (0, 2, 1, 3):
             nc.scalar.dma_start(
                 out=out_2[0, 4 * quad : 4 * quad + 4, :].bitcast(I32),
                 in_=out_scales[32 * quad : 32 * quad + 4, :].bitcast(I32),

@@ -18,8 +18,9 @@ ALU = mybir.AluOpType
 
 P = 128
 PACK = 4
-VECTOR_CHUNKS = ((0, 512), (512, 1152))
-SCALAR_CHUNKS = ((1152, 1664), (1664, 1920), (1920, 2048))
+SPLIT = 1280
+VECTOR_CHUNKS = ((0, 512), (512, 1024), (1024, SPLIT))
+SCALAR_CHUNKS = ((SPLIT, 1536), (1536, 1792), (1792, 1920), (1920, T))
 
 
 def tile_attend_gat_pl_sig_c_kernel(tc, qT, cT, doT, rw, qm, dom, offs, out_0, out_1, out_2):
@@ -56,6 +57,9 @@ def tile_attend_gat_pl_sig_c_kernel(tc, qT, cT, doT, rw, qm, dom, offs, out_0, o
         windows = [sb("window%d" % j, [P, T], F32) for j in range(PACK)]
         for j in range(PACK):
             nc.vector.memset(windows[j][:], 0.0)
+
+        warm = sb("warm", [P, 1], F32)
+        nc.scalar.activation(out=warm[:], in_=windows[0][:, 0:1], func=ACT.Sigmoid)
 
         grouped = {name: sb("grouped_" + name, [P, 512, PACK], BF16) for name in ("c", "ds", "pw")}
         names = ("c", "q", "do", "qm", "dom", "ds", "pw")
@@ -98,7 +102,7 @@ def tile_attend_gat_pl_sig_c_kernel(tc, qT, cT, doT, rw, qm, dom, offs, out_0, o
             nc.vector.tensor_copy(out=grouped["c"][:, :, j], in_=pool_planes[j][:].indirect(offsets[:]))
         quantize("c")
         deal(nc.vector.tensor_copy, "q", 0, "dealt_low")
-        deal(nc.vector.tensor_copy, "q", 1, "dealt_high")
+        deal(nc.scalar.copy, "q", 1, "dealt_mid")
         quantize_dealt("q", 0, 2)
         quantize_dealt("q", 2, 2)
         deal(nc.vector.tensor_copy, "do", 0, "dealt_low")
@@ -153,16 +157,7 @@ def tile_attend_gat_pl_sig_c_kernel(tc, qT, cT, doT, rw, qm, dom, offs, out_0, o
         quantize_dealt("dom", 2, 2)
 
         grad_sb = [sb("grad_sb%d" % j, [P, N], F32) for j in range(PACK)]
-        chunks = VECTOR_CHUNKS + SCALAR_CHUNKS
         out_rows = out_0.rearrange("(p j) t -> j p t", j=PACK)
-
-        def round_plane(copy, j, c):
-            dst = pair_view(c)[:, j // 2, :].rearrange("p (t e) -> p t e", e=2)
-            src = windows[j][:, c[0] : c[1]]
-            if j == 2 and c == spans[0]:
-                copy(out=dst, in_=src.unsqueeze(2).to_broadcast([P, c[1] - c[0], 2]))
-            else:
-                copy(out=dst[:, :, j % 2], in_=src)
 
         def product(j):
             grad = psum.tile([P, N], F32, name="grad%d" % j, tag="bank%d" % j)
@@ -174,60 +169,66 @@ def tile_attend_gat_pl_sig_c_kernel(tc, qT, cT, doT, rw, qm, dom, offs, out_0, o
 
         for j in range(PACK):
             product(j)
-        spans = ((0, VECTOR_CHUNKS[-1][1]), (SCALAR_CHUNKS[0][0], T))
-        freed = ("codes_pw", "codes_dom")
-        pairs = {s: sb("pairs%d" % s[0], [P, 2, (s[1] - s[0]) * 2], BF16, tag) for s, tag in zip(spans, freed)}
+        pairs = sb("pairs", [P, 2, SPLIT * 2], BF16, "codes_pw")
+        rows = sb("rows", [P, PACK, T - SPLIT], BF16, "codes_dom")
 
-        def pair_view(c):
-            s = spans[0] if c[0] < spans[0][1] else spans[1]
-            return pairs[s][:, :, 2 * (c[0] - s[0]) : 2 * (c[1] - s[0])]
+        def pair_lanes(j, c):
+            return pairs[:, j // 2, 2 * c[0] : 2 * c[1]].rearrange("p (t e) -> p t e", e=2)
 
         for j in range(PACK):
             nc.vector.tensor_copy(out=windows[j][:].indirect(offsets[:]), in_=grad_sb[j][:])
             nc.sync.dma_start(out=out_rows[j], in_=windows[j][:])
-            if j < PACK - 1:
-                for c in spans:
-                    round_plane(nc.scalar.copy, j, c)
+            if j < 2:
+                nc.scalar.copy(out=pair_lanes(j, (0, SPLIT))[:, :, j], in_=windows[j][:, 0:SPLIT])
+            if j == 2:
+                nc.scalar.copy(
+                    out=pair_lanes(j, (0, SPLIT)), in_=windows[j][:, 0:SPLIT].unsqueeze(2).to_broadcast([P, SPLIT, 2])
+                )
+            nc.scalar.copy(out=rows[:, j, :], in_=windows[j][:, SPLIT:T])
 
+        chunks = VECTOR_CHUNKS + SCALAR_CHUNKS
         out_grouped = {c: sb("out_grouped%d" % c[0], [P, (c[1] - c[0]) * PACK], BF16) for c in chunks}
         out_codes = sb("out_codes", [P, T], U32)
-        out_scales = sb("out_scales", [P, T], U8)
+        out_scales = sb("out_scales", [P, T // PACK], U8)
         words_dram = out_1[0].rearrange("p t l -> p (t l)").bitcast(I32)
 
-        def weave(copy, c):
-            src = pair_view(c).bitcast(F32).rearrange("p u t -> p t u")
+        def weave_pairs(c):
+            src = pairs[:, :, 2 * c[0] : 2 * c[1]].bitcast(F32).rearrange("p u t -> p t u")
             dst = out_grouped[c][:].bitcast(F32).rearrange("p (t u) -> p t u", u=2)
-            copy(out=dst, in_=src)
+            nc.vector.tensor_copy(out=dst, in_=src)
+
+        def weave_rows(c):
+            src = rows[:, :, c[0] - SPLIT : c[1] - SPLIT].rearrange("p j (c i) -> p c j i", i=4)
+            dst = out_grouped[c][:].rearrange("p (c i j) -> p c j i", i=4, j=PACK)
+            nc.scalar.copy(out=dst, in_=src)
 
         def quantize_out(c):
-            lo = c[0]
-            for width in (512, 256, 128):
-                if c[1] - lo >= width:
-                    nc.vector.quantize_mx(
-                        out=out_codes[:, lo : lo + width].bitcast(E4M3),
-                        scales=out_scales[:, lo : lo + width],
-                        in_=out_grouped[c][:, PACK * (lo - c[0]) : PACK * (lo - c[0] + width)],
-                    )
-                    lo = lo + width
+            for lo in range(c[0], c[1], 256):
+                hi = min(lo + 256, c[1])
+                quarter, col = divmod(lo, T // PACK)
+                nc.vector.quantize_mx(
+                    out=out_codes[:, lo:hi].bitcast(E4M3),
+                    scales=out_scales[4 * quarter : P, col : col + hi - lo],
+                    in_=out_grouped[c][:, PACK * (lo - c[0]) : PACK * (hi - c[0])],
+                )
 
         def store_words(lo, hi):
             nc.sync.dma_start(out=words_dram[:, lo:hi], in_=out_codes[:, lo:hi].bitcast(I32))
 
         for c in VECTOR_CHUNKS:
-            round_plane(nc.vector.tensor_copy, 3, c)
+            nc.vector.tensor_copy(out=pair_lanes(3, c)[:, :, 1], in_=windows[3][:, c[0] : c[1]])
         for c in VECTOR_CHUNKS:
-            weave(nc.vector.tensor_copy, c)
-        round_plane(nc.scalar.copy, 3, spans[1])
+            weave_pairs(c)
         for c in SCALAR_CHUNKS:
-            weave(nc.scalar.copy, c)
-        for c in chunks[:3]:
+            weave_rows(c)
+        stored = 0
+        for c in chunks:
             quantize_out(c)
-            store_words(c[0], c[1])
-        for c in chunks[3:]:
-            quantize_out(c)
-        store_words(chunks[3][0], T)
-        for quad in (0, 2, 1, 3):
-            nc.scalar.dma_start(
-                out=out_2[0, 4 * quad : 4 * quad + 4, :].bitcast(I32),
-                in_=out_scales[32 * quad : 32 * quad + 4, :].bitcast(I32),
+            if c[1] in (512, 1024, 1536, 1792, T):
+                store_words(stored, c[1])
+                stored = c[1]
+        for queue, quad in zip((nc.scalar, nc.scalar, nc.sync, nc.scalar), (0, 2, 1, 3)):
+            queue.dma_start(
+                out=out_2[0, 4 * quad : 4 * quad + 4, :].bitcast(I32).rearrange("f (u c) -> u f c", u=PACK),
+                in_=out_scales[32 * quad : 32 * quad + 16, :].bitcast(I32),
             )

@@ -63,36 +63,41 @@ def tile_attend_gat_pl_sig_c_kernel(tc, qT, cT, doT, rw, qm, dom, offs, out_0, o
 
         grouped = {name: sb("grouped_" + name, [P, 512, PACK], BF16) for name in ("c", "ds", "pw")}
         names = ("c", "q", "do", "qm", "dom", "ds", "pw")
-        codes = {name: sb("codes_" + name, [P, 512], U32) for name in names}
+        codes = {name: sb("codes_" + name, [P, 512], U32)[:] for name in names if name != "qm"}
+        codes["qm"] = sb("codes_qm", [P, P], U32)[:]
         scales = {name: sb("scales_" + name, [P, 512], U8) for name in names}
         dealt = {}
         fmt = {"c": E4M3, "q": E4M3, "do": E5M2, "qm": E4M3, "dom": E5M2, "ds": E5M2, "pw": E4M3}
 
         def quantize(name):
-            nc.vector.quantize_mx(out=codes[name][:].bitcast(fmt[name]), scales=scales[name][:], in_=flat(grouped[name]))
+            nc.vector.quantize_mx(out=codes[name].bitcast(fmt[name]), scales=scales[name][:], in_=flat(grouped[name]))
 
-        def deal(copy, name, half, tag):
-            dealt[name, half] = sb("dealt_%s%d" % (name, half), [P, 2 * P, PACK], BF16, tag)
-            dst = dealt[name, half][:].rearrange("p (t m) j -> p m j t", t=2)
+        def deal(copy, name, half, rows=slice(0, P)):
+            dst = dealt[name, half].rearrange("p (t m j) -> p m j t", t=2, j=PACK)
             src = raw[name][:].rearrange("p j (m t) -> p m j t", t=PACK)
-            copy(out=dst, in_=src[:, :, :, 2 * half : 2 * half + 2])
+            copy(out=dst[:, rows], in_=src[:, rows, :, 2 * half : 2 * half + 2])
+
+        def code_columns(name, first, count):
+            if name == "qm" and first > 0:
+                return codes["qm_rest"][:, P * (first - 1) : P * (first - 1 + count)]
+            return codes[name][:, P * first : P * (first + count)]
 
         def quantize_dealt(name, first, count):
             cols = slice(P * first, P * (first + count))
             lo = PACK * P * (first % 2)
             nc.vector.quantize_mx(
-                out=codes[name][:, cols].bitcast(fmt[name]),
+                out=code_columns(name, first, count).bitcast(fmt[name]),
                 scales=scales[name][:, cols],
-                in_=flat(dealt[name, first // 2])[:, lo : lo + PACK * P * count],
+                in_=dealt[name, first // 2][:, lo : lo + PACK * P * count],
             )
 
         def mx(out, stat, tile_index, mov, start, stop):
             cols = slice(P * tile_index, P * (tile_index + 1))
             nc.tensor.matmul_mx(
                 out=out[:],
-                lhsT=codes[stat][:, cols].bitcast(fmt[stat]),
+                lhsT=code_columns(stat, tile_index, 1).bitcast(fmt[stat]),
                 lhsT_scale=scales[stat][:, cols],
-                rhs=codes[mov][:].bitcast(fmt[mov]),
+                rhs=codes[mov].bitcast(fmt[mov]),
                 rhs_scale=scales[mov][:],
                 start=start,
                 stop=stop,
@@ -101,12 +106,23 @@ def tile_attend_gat_pl_sig_c_kernel(tc, qT, cT, doT, rw, qm, dom, offs, out_0, o
         for j in range(PACK):
             nc.vector.tensor_copy(out=grouped["c"][:, :, j], in_=pool_planes[j][:].indirect(offsets[:]))
         quantize("c")
-        deal(nc.vector.tensor_copy, "q", 0, "dealt_low")
-        deal(nc.scalar.copy, "q", 1, "dealt_mid")
+        half_width = 2 * P * PACK
+        neg_pw_flat = sb("neg_pw", [P, PACK * N], F32)
+        neg_pw = neg_pw_flat[:].rearrange("p (t n) -> p t n", t=PACK)
+        dealt["q", 0] = sb("dealt_q0", [P, half_width], BF16, "dealt_low")[:]
+        dealt["q", 1] = sb("dealt_q1", [P, half_width], BF16)[:]
+        deal(nc.vector.tensor_copy, "q", 0)
+        deal(nc.scalar.copy, "q", 1)
         quantize_dealt("q", 0, 2)
         quantize_dealt("q", 2, 2)
-        deal(nc.vector.tensor_copy, "do", 0, "dealt_low")
-        deal(nc.vector.tensor_copy, "do", 1, "dealt_high")
+        dealt["do", 0] = sb("dealt_do0", [P, half_width], BF16, "dealt_low")[:]
+        straddle = neg_pw_flat[:, 7 * N // 4 : 15 * N // 4].bitcast(BF16).rearrange("p (t w) -> p t w", t=2)
+        dealt_do_late = straddle[:, :, 0 : P * PACK]
+        deal(nc.vector.tensor_copy, "do", 0)
+        nc.vector.tensor_copy(
+            out=dealt_do_late.rearrange("p t (m j) -> p m j t", j=PACK),
+            in_=raw["do"][:].rearrange("p j (m t) -> p m j t", t=PACK)[:, :, :, 2:4],
+        )
 
         score = [psum.tile([P, N], F32, name="score%d" % t, tag="bank%d" % t) for t in range(PACK)]
         dprob = [psum.tile([P, N], F32, name="dprob%d" % t, tag="bank%d" % (PACK + t)) for t in range(PACK)]
@@ -117,42 +133,57 @@ def tile_attend_gat_pl_sig_c_kernel(tc, qT, cT, doT, rw, qm, dom, offs, out_0, o
         for t in range(PACK):
             nc.scalar.activation(out=prob[t][:], in_=score[t][:], func=ACT.Sigmoid)
 
-        quantize_dealt("do", 0, 2)
-        quantize_dealt("do", 2, 2)
-        for t in range(PACK):
-            mx(dprob[t], "do", t, "c", True, True)
-
-        neg_pw = sb("neg_pw", [P, PACK, N], F32)
         neg_dq = sb("neg_dq", [P, PACK, N], F32)
-        for t in range(PACK):
-            nc.vector.tensor_scalar(
+
+        def gate_product(engine, t):
+            engine.tensor_scalar(
                 out=neg_pw[:, t, :], in0=prob[t][:], scalar1=gate[:, t : t + 1], scalar2=-1.0,
                 op0=ALU.mult, op1=ALU.mult,
             )
+
+        quantize_dealt("do", 0, 2)
+        gate_product(nc.vector, 0)
+        for t in (2, 3):
+            nc.vector.quantize_mx(
+                out=codes["do"][:, P * t : P * (t + 1)].bitcast(E5M2),
+                scales=scales["do"][:, P * t : P * (t + 1)],
+                in_=dealt_do_late[:, t - 2, :],
+            )
+        for t in range(PACK):
+            mx(dprob[t], "do", t, "c", True, True)
+        for t in range(1, PACK):
+            gate_product(nc.gpsimd, t)
         for t in range(PACK):
             nc.vector.scalar_tensor_tensor(
                 out=neg_dq[:, t, :], in0=prob[t][:], scalar=1.0, in1=dprob[t][:],
                 op0=ALU.subtract, op1=ALU.mult,
             )
 
-        def runs(t):
-            return t[:].rearrange("p t (c i) -> p c t i", i=2)
+        def runs(ap):
+            return ap.rearrange("p t (c i) -> p c t i", i=2)
 
         def woven(t):
             return t[:].rearrange("p (c i) t -> p c t i", i=2)
 
-        deal(nc.scalar.copy, "qm", 0, "dealt_high")
+        whole = sb("dealt_qm", [P, 2 * half_width], BF16, "dealt_low")
+        dealt["qm", 0] = whole[:, 0:half_width]
+        dealt["qm", 1] = whole[:, half_width : 2 * half_width]
+        dealt["dom", 0] = sb("dealt_dom0", [P, half_width], BF16, "prob3")[:]
+        deal(nc.scalar.copy, "qm", 0)
+        deal(nc.scalar.copy, "qm", 1)
         nc.scalar.activation(out=woven(grouped["pw"]), in_=runs(neg_pw), func=ACT.Copy, scale=-1.0)
-        deal(nc.scalar.copy, "dom", 0, "prob2")
+        deal(nc.scalar.copy, "dom", 0)
+        nc.vector.tensor_tensor(out=woven(grouped["ds"]), in0=runs(neg_dq[:]), in1=runs(neg_pw), op=ALU.mult)
+        dealt["dom", 1] = sb("dealt_dom1", [P, half_width], BF16, "neg_dq")[:]
+        deal(nc.scalar.copy, "dom", 1, slice(0, P // 2))
         quantize_dealt("qm", 0, 1)
-        nc.vector.tensor_tensor(out=woven(grouped["ds"]), in0=runs(neg_dq), in1=runs(neg_pw), op=ALU.mult)
+        quantize("ds")
         quantize("pw")
         quantize_dealt("dom", 0, 1)
-        quantize("ds")
-        deal(nc.scalar.copy, "qm", 1, "prob3")
-        deal(nc.scalar.copy, "dom", 1, "neg_dq")
-        quantize_dealt("qm", 1, 1)
         quantize_dealt("dom", 1, 1)
+        deal(nc.vector.tensor_copy, "dom", 1, slice(P // 2, P))
+        codes["qm_rest"] = sb("codes_qm_rest", [P, 3 * P], U32, "prob3")[:]
+        quantize_dealt("qm", 1, 1)
         quantize_dealt("qm", 2, 2)
         quantize_dealt("dom", 2, 2)
 
@@ -161,7 +192,7 @@ def tile_attend_gat_pl_sig_c_kernel(tc, qT, cT, doT, rw, qm, dom, offs, out_0, o
 
         def product(j):
             grad = psum.tile([P, N], F32, name="grad%d" % j, tag="bank%d" % j)
-            passes = (("dom", "pw"), ("qm", "ds"))
+            passes = (("qm", "ds"), ("dom", "pw"))
             first, last = passes if j == 0 else passes[::-1]
             mx(grad, first[0], j, first[1], True, False)
             mx(grad, last[0], j, last[1], False, True)

@@ -36,7 +36,6 @@ def tile_attend_gat_pl_sig_c_kernel(tc, qT, cT, doT, rw, qm, dom, offs, out_0, o
             return t[:].rearrange("p w j -> p (w j)")
 
         offsets = keep.tile([P, N // 16], U16, name="offsets")
-        nc.sync.dma_start(offsets[:], offs)
 
         pool_planes = [sb("pool%d" % j, [P, T], F32) for j in range(PACK)]
         c_rows = cT.rearrange("(p j) t -> j p t", j=PACK)
@@ -48,6 +47,8 @@ def tile_attend_gat_pl_sig_c_kernel(tc, qT, cT, doT, rw, qm, dom, offs, out_0, o
 
         for j in range(PACK):
             nc.sync.dma_start(out=pool_planes[j][:], in_=c_rows[j])
+            if j == 0:
+                nc.sync.dma_start(offsets[:], offs)
         load("q", qT)
         load("do", doT)
         nc.sync.dma_start(out=gate[:], in_=rw[0].rearrange("(p t) o -> p (t o)", t=PACK))
@@ -160,17 +161,19 @@ def tile_attend_gat_pl_sig_c_kernel(tc, qT, cT, doT, rw, qm, dom, offs, out_0, o
             )
 
         def runs(ap):
-            return ap.rearrange("p t (c i) -> p c t i", i=2)
+            return ap.rearrange("p t (c i) -> p c t i", i=4)
 
         def woven(t):
-            return t[:].rearrange("p (c i) t -> p c t i", i=2)
+            return t[:].rearrange("p (c i) t -> p c t i", i=4)
 
         whole = sb("dealt_qm", [P, 2 * half_width], BF16, "dealt_low")
         dealt["qm", 0] = whole[:, 0:half_width]
         dealt["qm", 1] = whole[:, half_width : 2 * half_width]
         dealt["dom", 0] = sb("dealt_dom0", [P, half_width], BF16, "prob3")[:]
-        deal(nc.scalar.copy, "qm", 0)
-        deal(nc.scalar.copy, "qm", 1)
+        nc.scalar.copy(
+            out=whole[:].rearrange("p (t m j) -> p m j t", t=PACK, j=PACK),
+            in_=raw["qm"][:].rearrange("p j (m t) -> p m j t", t=PACK),
+        )
         nc.scalar.activation(out=woven(grouped["pw"]), in_=runs(neg_pw), func=ACT.Copy, scale=-1.0)
         deal(nc.scalar.copy, "dom", 0)
         nc.vector.tensor_tensor(out=woven(grouped["ds"]), in0=runs(neg_dq[:]), in1=runs(neg_pw), op=ALU.mult)

@@ -59,9 +59,6 @@ def tile_attend_gat_pl_sig_c_kernel(tc, qT, cT, doT, rw, qm, dom, offs, out_0, o
         for j in range(PACK):
             nc.vector.memset(windows[j][:], 0.0)
 
-        warm = sb("warm", [P, 1], F32)
-        nc.scalar.activation(out=warm[:], in_=windows[0][:, 0:1], func=ACT.Sigmoid)
-
         grouped = {name: sb("grouped_" + name, [P, 512, PACK], BF16) for name in ("c", "ds", "pw")}
         names = ("c", "q", "do", "qm", "dom", "ds", "pw")
         codes = {name: sb("codes_" + name, [P, 512], U32)[:] for name in names if name != "qm"}
@@ -113,7 +110,7 @@ def tile_attend_gat_pl_sig_c_kernel(tc, qT, cT, doT, rw, qm, dom, offs, out_0, o
         dealt["q", 0] = sb("dealt_q0", [P, half_width], BF16, "dealt_low")[:]
         dealt["q", 1] = sb("dealt_q1", [P, half_width], BF16)[:]
         deal(nc.vector.tensor_copy, "q", 0)
-        deal(nc.scalar.copy, "q", 1)
+        deal(nc.vector.tensor_copy, "q", 1)
         quantize_dealt("q", 0, 2)
         quantize_dealt("q", 2, 2)
         dealt["do", 0] = sb("dealt_do0", [P, half_width], BF16, "dealt_low")[:]

@@ -39,7 +39,9 @@ def tile_attend_gat_pl_sig_c_kernel(tc, qT, cT, doT, rw, qm, dom, offs, out_0, o
 
         pool_planes = [sb("pool%d" % j, [P, T], F32) for j in range(PACK)]
         c_rows = cT.rearrange("(p j) t -> j p t", j=PACK)
-        raw = {name: sb("raw_" + name, [P, PACK, 512], F32) for name in ("q", "do", "qm", "dom")}
+        raw = {name: sb("raw_" + name, [P, PACK, 512], F32) for name in ("q", "do", "dom")}
+        qm_bytes = sb("qm_bytes", [P, PACK * 512], F32)
+        raw["qm"] = qm_bytes[:].rearrange("p (j w) -> p j w", j=PACK)
         gate = sb("gate", [P, PACK], F32)
 
         def load(name, src):
@@ -59,13 +61,18 @@ def tile_attend_gat_pl_sig_c_kernel(tc, qT, cT, doT, rw, qm, dom, offs, out_0, o
         for j in range(PACK):
             nc.vector.memset(windows[j][:], 0.0)
 
-        grouped = {name: sb("grouped_" + name, [P, 512, PACK], BF16) for name in ("c", "ds", "pw")}
-        names = ("c", "q", "do", "qm", "dom", "ds", "pw")
-        codes = {name: sb("codes_" + name, [P, 512], U32)[:] for name in names if name != "qm"}
-        codes["qm"] = sb("codes_qm", [P, P], U32)[:]
-        scales = {name: sb("scales_" + name, [P, 512], U8) for name in names}
+        grouped = {name: sb("grouped_" + name, [P, 512, PACK], BF16) for name in ("c",)}
+        codes = {name: sb("codes_" + name, [P, 512], U32)[:] for name in ("c", "qm", "dom")}
+        scales = {name: sb("scales_" + name, [P, 512], U8)[:] for name in ("c", "qm", "dom")}
+        for before, name in (("do", "ds"), ("q", "pw")):
+            both_codes = sb("codes_" + name, [P, 2 * N], U32)
+            both_scales = sb("scales_" + name, [P, 2 * N], U8)
+            for key, first in ((before, 0), (name + "_early", N // 2), (name, N)):
+                codes[key] = both_codes[:, first : first + N]
+                scales[key] = both_scales[:, first : first + N]
         dealt = {}
         fmt = {"c": E4M3, "q": E4M3, "do": E5M2, "qm": E4M3, "dom": E5M2, "ds": E5M2, "pw": E4M3}
+        fmt["ds_early"], fmt["pw_early"] = E5M2, E4M3
 
         def quantize(name):
             nc.vector.quantize_mx(out=codes[name].bitcast(fmt[name]), scales=scales[name][:], in_=flat(grouped[name]))
@@ -76,8 +83,6 @@ def tile_attend_gat_pl_sig_c_kernel(tc, qT, cT, doT, rw, qm, dom, offs, out_0, o
             copy(out=dst[:, rows], in_=src[:, rows, :, 2 * half : 2 * half + 2])
 
         def code_columns(name, first, count):
-            if name == "qm" and first > 0:
-                return codes["qm_rest"][:, P * (first - 1) : P * (first - 1 + count)]
             return codes[name][:, P * first : P * (first + count)]
 
         def quantize_dealt(name, first, count):
@@ -163,59 +168,97 @@ def tile_attend_gat_pl_sig_c_kernel(tc, qT, cT, doT, rw, qm, dom, offs, out_0, o
         def woven(t):
             return t[:].rearrange("p (c i) t -> p c t i", i=4)
 
-        whole = sb("dealt_qm", [P, 2 * half_width], BF16, "dealt_low")
-        dealt["qm", 0] = whole[:, 0:half_width]
-        dealt["qm", 1] = whole[:, half_width : 2 * half_width]
-        dealt["dom", 0] = sb("dealt_dom0", [P, half_width], BF16, "prob3")[:]
-        nc.scalar.copy(
-            out=whole[:].rearrange("p (t m j) -> p m j t", t=PACK, j=PACK),
-            in_=raw["qm"][:].rearrange("p j (m t) -> p m j t", t=PACK),
-        )
-        nc.scalar.activation(out=woven(grouped["pw"]), in_=runs(neg_pw), func=ACT.Copy, scale=-1.0)
-        deal(nc.scalar.copy, "dom", 0)
-        nc.vector.tensor_tensor(out=woven(grouped["ds"]), in0=runs(neg_dq[:]), in1=runs(neg_pw), op=ALU.mult)
-        dealt["dom", 1] = sb("dealt_dom1", [P, half_width], BF16, "neg_dq")[:]
-        deal(nc.scalar.copy, "dom", 1, slice(0, P // 2))
-        quantize_dealt("qm", 0, 1)
-        quantize("ds")
-        quantize("pw")
-        quantize_dealt("dom", 0, 1)
-        quantize_dealt("dom", 1, 1)
-        deal(nc.vector.tensor_copy, "dom", 1, slice(P // 2, P))
-        codes["qm_rest"] = sb("codes_qm_rest", [P, 3 * P], U32, "prob3")[:]
-        quantize_dealt("qm", 1, 1)
-        quantize_dealt("qm", 2, 2)
-        quantize_dealt("dom", 2, 2)
+        half = N // 2
+        halves = (slice(0, half), slice(half, N))
+        dealt["qm", 0] = sb("dealt_qm0", [P, half_width], BF16)[:]
+        stage = sb("stage", [P, 3 * N], BF16)
+        dealt["dom", 0] = stage[:, N : 3 * N]
+        reused = stage[:, 0 : 2 * N]
+        first_halves = sb("first_halves", [P, 4 * N], BF16)
+        woven_pw = [first_halves[:, 2 * N : 4 * N].rearrange("p (s t) -> p s t", t=PACK)] * 2
+        woven_ds = [first_halves[:, 0 : 2 * N].rearrange("p (s t) -> p s t", t=PACK), reused.rearrange("p (s t) -> p s t", t=PACK)]
 
-        grad_sb = [sb("grad_sb%d" % j, [P, N], F32) for j in range(PACK)]
-        out_rows = out_0.rearrange("(p j) t -> j p t", j=PACK)
+        def weave_pw(h):
+            nc.scalar.activation(out=woven(woven_pw[h]), in_=runs(neg_pw[:, :, halves[h]]), func=ACT.Copy, scale=-1.0)
 
-        def product(j):
-            grad = psum.tile([P, N], F32, name="grad%d" % j, tag="bank%d" % j)
-            passes = (("qm", "ds"), ("dom", "pw"))
-            first, last = passes if j == 0 else passes[::-1]
+        def weave_ds(h):
+            nc.vector.tensor_tensor(
+                out=woven(woven_ds[h]), in0=runs(neg_dq[:, :, halves[h]]), in1=runs(neg_pw[:, :, halves[h]]), op=ALU.mult
+            )
+
+        def quantize_half(name, tiles, h):
+            nc.vector.quantize_mx(
+                out=codes[name][:, halves[h]].bitcast(fmt[name]), scales=scales[name][:, halves[h]], in_=flat(tiles[h])
+            )
+
+        def product(j, bank):
+            grad = psum.tile([P, N], F32, name="grad%d_%d" % (j, bank), tag="bank%d" % bank)
+            suffix = "_early" if bank == PACK else ""
+            passes = (("dom", "pw" + suffix), ("qm", "ds" + suffix))
+            first, last = passes if bank == 0 else passes[::-1]
             mx(grad, first[0], j, first[1], True, False)
             mx(grad, last[0], j, last[1], False, True)
-            nc.scalar.copy(out=grad_sb[j][:], in_=grad[:])
+            return grad
 
-        for j in range(PACK):
-            product(j)
-        pairs = sb("pairs", [P, 2, SPLIT * 2], BF16, "codes_pw")
-        rows = sb("rows", [P, PACK, T - SPLIT], BF16, "codes_dom")
+        out_rows = out_0.rearrange("(p j) t -> j p t", j=PACK)
+        list_halves = (offsets[:, 0 : half // 16], offsets[:, half // 16 : N // 16])
+
+        deal(nc.scalar.copy, "qm", 0)
+        weave_pw(0)
+        deal(nc.scalar.copy, "dom", 0)
+        quantize_dealt("qm", 0, 1)
+        weave_ds(0)
+        quantize_half("pw", woven_pw, 0)
+        weave_pw(1)
+        quantize_half("ds", woven_ds, 0)
+        quantize_dealt("qm", 1, 1)
+        quantize_dealt("dom", 0, 1)
+        dealt["qm", 1] = first_halves[:, N // 2 : 5 * N // 2]
+        deal(nc.scalar.copy, "qm", 1, slice(0, P // 2))
+        early = product(0, PACK)
+        grad_early = sb("grad_early", [P, half], F32)
+        nc.scalar.copy(out=grad_early[:], in_=early[:, halves[1]])
+        weave_ds(1)
+        quantize_half("pw", woven_pw, 1)
+        deal(nc.scalar.copy, "qm", 1, slice(P // 2, P))
+        quantize_dealt("dom", 1, 1)
+        quantize_half("ds", woven_ds, 1)
+        nc.vector.tensor_copy(out=windows[0][:].indirect(list_halves[0]), in_=grad_early[:])
+        dealt["dom", 1] = reused
+        deal(nc.scalar.copy, "dom", 1)
+        grad_late = sb("grad_late", [P, half], F32)
+        nc.scalar.copy(out=grad_late[:], in_=product(0, 0)[:, halves[1]])
+        quantize_dealt("qm", 2, 2)
+        quantize_dealt("dom", 2, 2)
+        nc.vector.tensor_copy(out=windows[0][:].indirect(list_halves[1]), in_=grad_late[:])
+        nc.sync.dma_start(out=out_rows[0], in_=windows[0][:])
+        grad_sb = {j: sb("grad_sb%d" % j, [P, N], F32)[:] for j in range(1, PACK)}
+        for j in range(1, PACK):
+            nc.scalar.copy(out=grad_sb[j], in_=product(j, j)[:])
 
         def pair_lanes(j, c):
             return pairs[:, j // 2, 2 * c[0] : 2 * c[1]].rearrange("p (t e) -> p t e", e=2)
 
-        for j in range(PACK):
-            nc.vector.tensor_copy(out=windows[j][:].indirect(offsets[:]), in_=grad_sb[j][:])
-            nc.sync.dma_start(out=out_rows[j], in_=windows[j][:])
+        def round_pairs(j):
             if j < 2:
                 nc.scalar.copy(out=pair_lanes(j, (0, SPLIT))[:, :, j], in_=windows[j][:, 0:SPLIT])
             if j == 2:
                 nc.scalar.copy(
                     out=pair_lanes(j, (0, SPLIT)), in_=windows[j][:, 0:SPLIT].unsqueeze(2).to_broadcast([P, SPLIT, 2])
                 )
+
+        def round_rows(j):
             nc.scalar.copy(out=rows[:, j, :], in_=windows[j][:, SPLIT:T])
+
+        pairs = sb("pairs", [P, 2, SPLIT * 2], BF16, "codes_pw")
+        rows = sb("rows", [P, PACK, T - SPLIT], BF16, "codes_dom")
+        round_pairs(0)
+        round_rows(0)
+        for j in range(1, PACK):
+            nc.vector.tensor_copy(out=windows[j][:].indirect(offsets[:]), in_=grad_sb[j])
+            nc.sync.dma_start(out=out_rows[j], in_=windows[j][:])
+            round_pairs(j)
+            round_rows(j)
 
         chunks = VECTOR_CHUNKS + SCALAR_CHUNKS
         out_grouped = {c: sb("out_grouped%d" % c[0], [P, (c[1] - c[0]) * PACK], BF16) for c in chunks}

@@ -18,9 +18,13 @@ ALU = mybir.AluOpType
 
 P = 128
 PACK = 4
-SPLIT = 1280
+HALF = N // 2
+QUARTER = T // PACK
+SPLIT = 1152
 VECTOR_CHUNKS = ((0, 512), (512, 1024), (1024, SPLIT))
 SCALAR_CHUNKS = ((SPLIT, 1536), (1536, 1792), (1792, 1920), (1920, T))
+STORE_ENDS = (512, 1024, 1536, T)
+FORMATS = {"c": E4M3, "q": E4M3, "do": E5M2, "qm": E4M3, "dom": E5M2, "ds": E5M2, "pw": E4M3}
 
 
 def tile_attend_gat_pl_sig_c_kernel(tc, qT, cT, doT, rw, qm, dom, offs, out_0, out_1, out_2):
@@ -32,16 +36,12 @@ def tile_attend_gat_pl_sig_c_kernel(tc, qT, cT, doT, rw, qm, dom, offs, out_0, o
         def sb(name, shape, dtype, tag=None):
             return keep.tile(shape, dtype, name=name, tag=tag or name, align_bytes=64)
 
-        def flat(t):
-            return t[:].rearrange("p w j -> p (w j)")
-
         offsets = keep.tile([P, N // 16], U16, name="offsets")
+        list_halves = [offsets[:, h * HALF // 16 : (h + 1) * HALF // 16] for h in range(2)]
 
         pool_planes = [sb("pool%d" % j, [P, T], F32) for j in range(PACK)]
         c_rows = cT.rearrange("(p j) t -> j p t", j=PACK)
-        raw = {name: sb("raw_" + name, [P, PACK, 512], F32) for name in ("q", "do", "dom")}
-        qm_bytes = sb("qm_bytes", [P, PACK * 512], F32)
-        raw["qm"] = qm_bytes[:].rearrange("p (j w) -> p j w", j=PACK)
+        raw = {name: sb("raw_" + name, [P, PACK, 512], F32) for name in ("q", "do", "qm", "dom")}
         gate = sb("gate", [P, PACK], F32)
 
         def load(name, src):
@@ -61,245 +61,195 @@ def tile_attend_gat_pl_sig_c_kernel(tc, qT, cT, doT, rw, qm, dom, offs, out_0, o
         for j in range(PACK):
             nc.vector.memset(windows[j][:], 0.0)
 
-        grouped = {name: sb("grouped_" + name, [P, 512, PACK], BF16) for name in ("c",)}
-        codes = {name: sb("codes_" + name, [P, 512], U32)[:] for name in ("c", "qm", "dom")}
-        scales = {name: sb("scales_" + name, [P, 512], U8)[:] for name in ("c", "qm", "dom")}
-        for before, name in (("do", "ds"), ("q", "pw")):
-            both_codes = sb("codes_" + name, [P, 2 * N], U32)
-            both_scales = sb("scales_" + name, [P, 2 * N], U8)
-            for key, first in ((before, 0), (name + "_early", N // 2), (name, N)):
-                codes[key] = both_codes[:, first : first + N]
-                scales[key] = both_scales[:, first : first + N]
-        dealt = {}
-        fmt = {"c": E4M3, "q": E4M3, "do": E5M2, "qm": E4M3, "dom": E5M2, "ds": E5M2, "pw": E4M3}
-        fmt["ds_early"], fmt["pw_early"] = E5M2, E4M3
+        codes = {name: sb("codes_" + name, [P, 512], U32) for name in FORMATS}
+        scales = {name: sb("scales_" + name, [P, 512], U8) for name in FORMATS}
+        half_width = HALF * PACK
+        laid_c = sb("laid_c", [P, N * PACK], BF16)
+        laid = {key: sb("laid_%s%d" % key, [P, half_width], BF16)[:] for key in (("q", 0), ("q", 1), ("do", 0), ("qm", 0), ("ds", 0))}
+        late_do = sb("late_do", [P, HALF * 2], F32)
+        laid["do", 1] = late_do[:].bitcast(BF16)
+        neg_gate = late_do[:, 0:PACK]
+        laid_pw = sb("laid_pw", [P, half_width], BF16)
+        laid["pw", 0] = laid["pw", 1] = laid["qm", 1] = laid_pw[:]
+        laid_dom = sb("laid_dom", [P, half_width], BF16)
+        laid["dom", 0] = laid["ds", 1] = laid["dom", 1] = laid_dom[:]
 
-        def quantize(name):
-            nc.vector.quantize_mx(out=codes[name].bitcast(fmt[name]), scales=scales[name][:], in_=flat(grouped[name]))
-
-        def deal(copy, name, half, rows=slice(0, P)):
-            dst = dealt[name, half].rearrange("p (t m j) -> p m j t", t=2, j=PACK)
-            src = raw[name][:].rearrange("p j (m t) -> p m j t", t=PACK)
-            copy(out=dst[:, rows], in_=src[:, rows, :, 2 * half : 2 * half + 2])
-
-        def code_columns(name, first, count):
-            return codes[name][:, P * first : P * (first + count)]
-
-        def quantize_dealt(name, first, count):
-            cols = slice(P * first, P * (first + count))
-            lo = PACK * P * (first % 2)
+        def quantize(name, h):
+            cols = slice(h * HALF, (h + 1) * HALF)
             nc.vector.quantize_mx(
-                out=code_columns(name, first, count).bitcast(fmt[name]),
-                scales=scales[name][:, cols],
-                in_=dealt[name, first // 2][:, lo : lo + PACK * P * count],
+                out=codes[name][:, cols].bitcast(FORMATS[name]), scales=scales[name][:, cols], in_=laid[name, h]
             )
 
-        def mx(out, stat, tile_index, mov, start, stop):
+        def deal(copy, name, h):
+            dst = laid[name, h].rearrange("p (t m j) -> p m j t", t=2, j=PACK)
+            src = raw[name][:].rearrange("p j (m t) -> p m j t", t=PACK)
+            copy(out=dst, in_=src[:, :, :, 2 * h : 2 * h + 2])
+
+        def mx(out, stat, tile_index, mov, slots, start, stop):
             cols = slice(P * tile_index, P * (tile_index + 1))
             nc.tensor.matmul_mx(
-                out=out[:],
-                lhsT=code_columns(stat, tile_index, 1).bitcast(fmt[stat]),
+                out=out,
+                lhsT=codes[stat][:, cols].bitcast(FORMATS[stat]),
                 lhsT_scale=scales[stat][:, cols],
-                rhs=codes[mov].bitcast(fmt[mov]),
-                rhs_scale=scales[mov][:],
+                rhs=codes[mov][:, slots].bitcast(FORMATS[mov]),
+                rhs_scale=scales[mov][:, slots],
                 start=start,
                 stop=stop,
             )
 
+        whole = slice(0, N)
+        halves = (slice(0, HALF), slice(HALF, N))
+        c_lanes = laid_c[:].rearrange("p (s j) -> p s j", j=PACK)
         for j in range(PACK):
-            nc.vector.tensor_copy(out=grouped["c"][:, :, j], in_=pool_planes[j][:].indirect(offsets[:]))
-        quantize("c")
-        half_width = 2 * P * PACK
-        neg_pw_flat = sb("neg_pw", [P, PACK * N], F32)
-        neg_pw = neg_pw_flat[:].rearrange("p (t n) -> p t n", t=PACK)
-        dealt["q", 0] = sb("dealt_q0", [P, half_width], BF16, "dealt_low")[:]
-        dealt["q", 1] = sb("dealt_q1", [P, half_width], BF16)[:]
-        deal(nc.vector.tensor_copy, "q", 0)
-        deal(nc.vector.tensor_copy, "q", 1)
-        quantize_dealt("q", 0, 2)
-        quantize_dealt("q", 2, 2)
-        dealt["do", 0] = sb("dealt_do0", [P, half_width], BF16, "dealt_low")[:]
-        straddle = neg_pw_flat[:, 7 * N // 4 : 15 * N // 4].bitcast(BF16).rearrange("p (t w) -> p t w", t=2)
-        dealt_do_late = straddle[:, :, 0 : P * PACK]
-        deal(nc.vector.tensor_copy, "do", 0)
-        nc.vector.tensor_copy(
-            out=dealt_do_late.rearrange("p t (m j) -> p m j t", j=PACK),
-            in_=raw["do"][:].rearrange("p j (m t) -> p m j t", t=PACK)[:, :, :, 2:4],
-        )
+            nc.vector.tensor_copy(out=c_lanes[:, :, j], in_=pool_planes[j][:].indirect(offsets[:]))
+        nc.vector.quantize_mx(out=codes["c"][:].bitcast(E4M3), scales=scales["c"][:], in_=laid_c[:])
+        for name in ("q", "do"):
+            for h in range(2):
+                deal(nc.vector.tensor_copy, name, h)
+            for h in range(2):
+                quantize(name, h)
 
-        score = [psum.tile([P, N], F32, name="score%d" % t, tag="bank%d" % t) for t in range(PACK)]
-        dprob = [psum.tile([P, N], F32, name="dprob%d" % t, tag="bank%d" % (PACK + t)) for t in range(PACK)]
-        for t in range(PACK):
-            mx(score[t], "q", t, "c", True, True)
+        def bank(name, index, width):
+            return psum.tile([P, width], F32, name=name, tag="bank%d" % index)
 
+        score = [bank("score%d" % t, t, N) for t in range(PACK)]
+        dprob = [bank("dprob%d" % t, PACK + t, N) for t in range(PACK)]
         prob = [sb("prob%d" % t, [P, N], F32) for t in range(PACK)]
+        for t in range(PACK):
+            mx(score[t][:], "q", t, "c", whole, True, True)
+        for t in range(PACK):
+            mx(dprob[t][:], "do", t, "c", whole, True, True)
         for t in range(PACK):
             nc.scalar.activation(out=prob[t][:], in_=score[t][:], func=ACT.Sigmoid)
 
+        neg_pw = sb("neg_pw", [P, PACK, N], F32)
         neg_dq = sb("neg_dq", [P, PACK, N], F32)
-
-        def gate_product(engine, t):
-            engine.tensor_scalar(
-                out=neg_pw[:, t, :], in0=prob[t][:], scalar1=gate[:, t : t + 1], scalar2=-1.0,
-                op0=ALU.mult, op1=ALU.mult,
-            )
-
-        quantize_dealt("do", 0, 2)
-        gate_product(nc.vector, 0)
-        for t in (2, 3):
-            nc.vector.quantize_mx(
-                out=codes["do"][:, P * t : P * (t + 1)].bitcast(E5M2),
-                scales=scales["do"][:, P * t : P * (t + 1)],
-                in_=dealt_do_late[:, t - 2, :],
-            )
-        for t in range(PACK):
-            mx(dprob[t], "do", t, "c", True, True)
-        for t in range(1, PACK):
-            gate_product(nc.gpsimd, t)
+        nc.vector.tensor_scalar(
+            out=neg_pw[:, 0, :], in0=prob[0][:], scalar1=gate[:, 0:1], scalar2=-1.0, op0=ALU.mult, op1=ALU.mult
+        )
+        nc.gpsimd.tensor_scalar(out=neg_gate, in0=gate[:], scalar1=-1.0, scalar2=0.0, op0=ALU.mult, op1=ALU.add)
+        for h in range(2):
+            for t in range(1, PACK):
+                nc.gpsimd.tensor_scalar(
+                    out=neg_pw[:, t, halves[h]], in0=prob[t][:, halves[h]], scalar1=neg_gate[:, t : t + 1], scalar2=0.0,
+                    op0=ALU.mult, op1=ALU.add,
+                )
         for t in range(PACK):
             nc.vector.scalar_tensor_tensor(
-                out=neg_dq[:, t, :], in0=prob[t][:], scalar=1.0, in1=dprob[t][:],
-                op0=ALU.subtract, op1=ALU.mult,
+                out=neg_dq[:, t, :], in0=prob[t][:], scalar=1.0, in1=dprob[t][:], op0=ALU.subtract, op1=ALU.mult
             )
 
         def runs(ap):
             return ap.rearrange("p t (c i) -> p c t i", i=4)
 
-        def woven(t):
-            return t[:].rearrange("p (c i) t -> p c t i", i=4)
-
-        half = N // 2
-        halves = (slice(0, half), slice(half, N))
-        dealt["qm", 0] = sb("dealt_qm0", [P, half_width], BF16)[:]
-        stage = sb("stage", [P, 3 * N], BF16)
-        dealt["dom", 0] = stage[:, N : 3 * N]
-        reused = stage[:, 0 : 2 * N]
-        first_halves = sb("first_halves", [P, 4 * N], BF16)
-        woven_pw = [first_halves[:, 2 * N : 4 * N].rearrange("p (s t) -> p s t", t=PACK)] * 2
-        woven_ds = [first_halves[:, 0 : 2 * N].rearrange("p (s t) -> p s t", t=PACK), reused.rearrange("p (s t) -> p s t", t=PACK)]
+        def woven(ap):
+            return ap.rearrange("p (c i t) -> p c t i", i=4, t=PACK)
 
         def weave_pw(h):
-            nc.scalar.activation(out=woven(woven_pw[h]), in_=runs(neg_pw[:, :, halves[h]]), func=ACT.Copy, scale=-1.0)
+            nc.scalar.activation(out=woven(laid["pw", h]), in_=runs(neg_pw[:, :, halves[h]]), func=ACT.Copy, scale=-1.0)
 
         def weave_ds(h):
             nc.vector.tensor_tensor(
-                out=woven(woven_ds[h]), in0=runs(neg_dq[:, :, halves[h]]), in1=runs(neg_pw[:, :, halves[h]]), op=ALU.mult
+                out=woven(laid["ds", h]), in0=runs(neg_dq[:, :, halves[h]]), in1=runs(neg_pw[:, :, halves[h]]), op=ALU.mult
             )
 
-        def quantize_half(name, tiles, h):
-            nc.vector.quantize_mx(
-                out=codes[name][:, halves[h]].bitcast(fmt[name]), scales=scales[name][:, halves[h]], in_=flat(tiles[h])
-            )
-
-        def product(j, bank):
-            grad = psum.tile([P, N], F32, name="grad%d_%d" % (j, bank), tag="bank%d" % bank)
-            suffix = "_early" if bank == PACK else ""
-            passes = (("dom", "pw" + suffix), ("qm", "ds" + suffix))
-            first, last = passes if bank == 0 else passes[::-1]
-            mx(grad, first[0], j, first[1], True, False)
-            mx(grad, last[0], j, last[1], False, True)
+        def product(j, index, slots, first, last):
+            grad = bank("grad%d" % index, index, slots.stop - slots.start)
+            mx(grad[:], first[0], j, first[1], slots, True, False)
+            mx(grad[:], last[0], j, last[1], slots, False, True)
             return grad
 
+        by_keys, by_values = ("qm", "ds"), ("dom", "pw")
         out_rows = out_0.rearrange("(p j) t -> j p t", j=PACK)
-        list_halves = (offsets[:, 0 : half // 16], offsets[:, half // 16 : N // 16])
+        grad_sb = [sb("grad_sb%d" % j, [P, N], F32) for j in range(PACK)]
+
+        def scatter_half(j, h):
+            nc.scalar.activation(out=windows[j][:].indirect(list_halves[h]), in_=grad_sb[j][:, halves[h]], func=ACT.Copy)
+
+        def store(j):
+            nc.sync.dma_start(out=out_rows[j], in_=windows[j][:])
 
         deal(nc.scalar.copy, "qm", 0)
         weave_pw(0)
         deal(nc.scalar.copy, "dom", 0)
-        quantize_dealt("qm", 0, 1)
         weave_ds(0)
-        quantize_half("pw", woven_pw, 0)
+        quantize("qm", 0)
+        quantize("pw", 0)
         weave_pw(1)
-        quantize_half("ds", woven_ds, 0)
-        quantize_dealt("qm", 1, 1)
-        quantize_dealt("dom", 0, 1)
-        dealt["qm", 1] = first_halves[:, N // 2 : 5 * N // 2]
-        deal(nc.scalar.copy, "qm", 1, slice(0, P // 2))
-        early = product(0, PACK)
-        grad_early = sb("grad_early", [P, half], F32)
-        nc.scalar.copy(out=grad_early[:], in_=early[:, halves[1]])
+        quantize("ds", 0)
+        quantize("dom", 0)
+        nc.scalar.copy(out=grad_sb[0][:, halves[0]], in_=product(0, 0, halves[0], by_keys, by_values)[:])
+        scatter_half(0, 0)
         weave_ds(1)
-        quantize_half("pw", woven_pw, 1)
-        deal(nc.scalar.copy, "qm", 1, slice(P // 2, P))
-        quantize_dealt("dom", 1, 1)
-        quantize_half("ds", woven_ds, 1)
-        nc.vector.tensor_copy(out=windows[0][:].indirect(list_halves[0]), in_=grad_early[:])
-        dealt["dom", 1] = reused
-        deal(nc.scalar.copy, "dom", 1)
-        grad_late = sb("grad_late", [P, half], F32)
-        nc.scalar.copy(out=grad_late[:], in_=product(0, 0)[:, halves[1]])
-        quantize_dealt("qm", 2, 2)
-        quantize_dealt("dom", 2, 2)
-        nc.vector.tensor_copy(out=windows[0][:].indirect(list_halves[1]), in_=grad_late[:])
-        nc.sync.dma_start(out=out_rows[0], in_=windows[0][:])
-        grad_sb = {j: sb("grad_sb%d" % j, [P, N], F32)[:] for j in range(1, PACK)}
-        for j in range(1, PACK):
-            nc.scalar.copy(out=grad_sb[j], in_=product(j, j)[:])
+        quantize("pw", 1)
+        quantize("ds", 1)
+        nc.scalar.copy(out=grad_sb[0][:, halves[1]], in_=product(0, PACK, halves[1], by_values, by_keys)[:])
+        scatter_half(0, 1)
+        store(0)
+        grad1 = product(1, 1, whole, by_values, by_keys)
+        for name in ("qm", "dom"):
+            deal(nc.vector.tensor_copy, name, 1)
+        for name in ("qm", "dom"):
+            quantize(name, 1)
+        nc.vector.tensor_copy(out=grad_sb[1][:], in_=grad1[:])
+        nc.vector.tensor_copy(out=grad_sb[2][:], in_=product(2, 2, whole, by_keys, by_values)[:])
+        nc.vector.tensor_copy(out=windows[2][:].indirect(offsets[:]), in_=grad_sb[2][:])
+        store(2)
+        scatter_half(1, 0)
+        nc.scalar.copy(out=grad_sb[3][:], in_=product(3, 3, whole, by_keys, by_values)[:])
+        scatter_half(1, 1)
+        store(1)
+        for h in range(2):
+            scatter_half(3, h)
+        store(3)
 
-        def pair_lanes(j, c):
-            return pairs[:, j // 2, 2 * c[0] : 2 * c[1]].rearrange("p (t e) -> p t e", e=2)
+        pairs = sb("pairs", [P, 2, T * 2], BF16, "codes_pw")
 
-        def round_pairs(j):
-            if j < 2:
-                nc.scalar.copy(out=pair_lanes(j, (0, SPLIT))[:, :, j], in_=windows[j][:, 0:SPLIT])
-            if j == 2:
-                nc.scalar.copy(
-                    out=pair_lanes(j, (0, SPLIT)), in_=windows[j][:, 0:SPLIT].unsqueeze(2).to_broadcast([P, SPLIT, 2])
-                )
+        def pair_lanes(j, lo, hi):
+            return pairs[:, j // 2, 2 * lo : 2 * hi].rearrange("p (t e) -> p t e", e=2)
 
-        def round_rows(j):
-            nc.scalar.copy(out=rows[:, j, :], in_=windows[j][:, SPLIT:T])
-
-        pairs = sb("pairs", [P, 2, SPLIT * 2], BF16, "codes_pw")
-        rows = sb("rows", [P, PACK, T - SPLIT], BF16, "codes_dom")
-        round_pairs(0)
-        round_rows(0)
-        for j in range(1, PACK):
-            nc.vector.tensor_copy(out=windows[j][:].indirect(offsets[:]), in_=grad_sb[j])
-            nc.sync.dma_start(out=out_rows[j], in_=windows[j][:])
-            round_pairs(j)
-            round_rows(j)
+        nc.vector.tensor_copy(out=pair_lanes(0, 0, T)[:, :, 0], in_=windows[0][:])
+        nc.vector.tensor_copy(out=pair_lanes(2, 0, SPLIT)[:, :, 0], in_=windows[2][:, 0:SPLIT])
+        nc.vector.tensor_copy(
+            out=pair_lanes(2, SPLIT, T), in_=windows[2][:, SPLIT:T].unsqueeze(2).to_broadcast([P, T - SPLIT, 2])
+        )
+        nc.vector.tensor_copy(out=pair_lanes(1, 0, T)[:, :, 1], in_=windows[1][:])
 
         chunks = VECTOR_CHUNKS + SCALAR_CHUNKS
-        out_grouped = {c: sb("out_grouped%d" % c[0], [P, (c[1] - c[0]) * PACK], BF16) for c in chunks}
+        out_laid = {c: sb("out_laid%d" % c[0], [P, (c[1] - c[0]) * PACK], BF16) for c in chunks}
         out_codes = sb("out_codes", [P, T], U32)
-        out_scales = sb("out_scales", [P, T // PACK], U8)
+        out_scales = sb("out_scales", [P, QUARTER], U8)
         words_dram = out_1[0].rearrange("p t l -> p (t l)").bitcast(I32)
 
-        def weave_pairs(c):
+        def weave_pairs(copy, c):
             src = pairs[:, :, 2 * c[0] : 2 * c[1]].bitcast(F32).rearrange("p u t -> p t u")
-            dst = out_grouped[c][:].bitcast(F32).rearrange("p (t u) -> p t u", u=2)
-            nc.vector.tensor_copy(out=dst, in_=src)
-
-        def weave_rows(c):
-            src = rows[:, :, c[0] - SPLIT : c[1] - SPLIT].rearrange("p j (c i) -> p c j i", i=4)
-            dst = out_grouped[c][:].rearrange("p (c i j) -> p c j i", i=4, j=PACK)
-            nc.scalar.copy(out=dst, in_=src)
+            copy(out=out_laid[c][:].bitcast(F32).rearrange("p (t u) -> p t u", u=2), in_=src)
 
         def quantize_out(c):
-            for lo in range(c[0], c[1], 256):
-                hi = min(lo + 256, c[1])
-                quarter, col = divmod(lo, T // PACK)
-                nc.vector.quantize_mx(
-                    out=out_codes[:, lo:hi].bitcast(E4M3),
-                    scales=out_scales[4 * quarter : P, col : col + hi - lo],
-                    in_=out_grouped[c][:, PACK * (lo - c[0]) : PACK * (hi - c[0])],
-                )
-
-        def store_words(lo, hi):
-            nc.sync.dma_start(out=words_dram[:, lo:hi], in_=out_codes[:, lo:hi].bitcast(I32))
+            lo = c[0]
+            for hi in range(c[0] + P, c[1] + 1, P):
+                if hi % 256 == 0 or hi == c[1]:
+                    quarter, col = divmod(lo, QUARTER)
+                    nc.vector.quantize_mx(
+                        out=out_codes[:, lo:hi].bitcast(E4M3),
+                        scales=out_scales[4 * quarter : P, col : col + hi - lo],
+                        in_=out_laid[c][:, PACK * (lo - c[0]) : PACK * (hi - c[0])],
+                    )
+                    lo = hi
 
         for c in VECTOR_CHUNKS:
-            nc.vector.tensor_copy(out=pair_lanes(3, c)[:, :, 1], in_=windows[3][:, c[0] : c[1]])
+            nc.vector.tensor_copy(out=pair_lanes(3, *c)[:, :, 1], in_=windows[3][:, c[0] : c[1]])
+        for lo, hi in ((SPLIT, SCALAR_CHUNKS[0][1]), (SCALAR_CHUNKS[0][1], T)):
+            nc.scalar.copy(out=pair_lanes(3, lo, hi)[:, :, 1], in_=windows[3][:, lo:hi])
         for c in VECTOR_CHUNKS:
-            weave_pairs(c)
+            weave_pairs(nc.vector.tensor_copy, c)
         for c in SCALAR_CHUNKS:
-            weave_rows(c)
+            weave_pairs(nc.scalar.copy, c)
         stored = 0
         for c in chunks:
             quantize_out(c)
-            if c[1] in (512, 1024, 1536, 1792, T):
-                store_words(stored, c[1])
+            if c[1] in STORE_ENDS:
+                nc.sync.dma_start(out=words_dram[:, stored : c[1]], in_=out_codes[:, stored : c[1]].bitcast(I32))
                 stored = c[1]
         for queue, quad in zip((nc.scalar, nc.scalar, nc.sync, nc.scalar), (0, 2, 1, 3)):
             queue.dma_start(

@@ -20,9 +20,9 @@ P = 128
 PACK = 4
 HALF = N // 2
 QUARTER = T // PACK
-SPLIT = 1152
-VECTOR_CHUNKS = ((0, 512), (512, 1024), (1024, SPLIT))
-SCALAR_CHUNKS = ((SPLIT, 1536), (1536, 1792), (1792, 1920), (1920, T))
+SPLIT = 768
+VECTOR_CHUNKS = ((0, 512), (512, SPLIT))
+SCALAR_CHUNKS = ((SPLIT, 1024), (1024, 1536), (1536, 1792), (1792, 1920), (1920, T))
 STORE_ENDS = (512, 1024, 1536, T)
 FORMATS = {"c": E4M3, "q": E4M3, "do": E5M2, "qm": E4M3, "dom": E5M2, "ds": E5M2, "pw": E4M3}
 
@@ -65,14 +65,15 @@ def tile_attend_gat_pl_sig_c_kernel(tc, qT, cT, doT, rw, qm, dom, offs, out_0, o
         scales = {name: sb("scales_" + name, [P, 512], U8) for name in FORMATS}
         half_width = HALF * PACK
         laid_c = sb("laid_c", [P, N * PACK], BF16)
-        laid = {key: sb("laid_%s%d" % key, [P, half_width], BF16)[:] for key in (("q", 0), ("q", 1), ("do", 0), ("qm", 0), ("ds", 0))}
+        own_bytes = (("q", 0), ("q", 1), ("do", 0), ("qm", 0), ("ds", 0), ("pw", 0), ("dom", 1))
+        laid = {key: sb("laid_%s%d" % key, [P, half_width], BF16)[:] for key in own_bytes}
         late_do = sb("late_do", [P, HALF * 2], F32)
         laid["do", 1] = late_do[:].bitcast(BF16)
         neg_gate = late_do[:, 0:PACK]
-        laid_pw = sb("laid_pw", [P, half_width], BF16)
-        laid["pw", 0] = laid["pw", 1] = laid["qm", 1] = laid_pw[:]
-        laid_dom = sb("laid_dom", [P, half_width], BF16)
-        laid["dom", 0] = laid["ds", 1] = laid["dom", 1] = laid_dom[:]
+        stage = sb("stage", [P, 2 * half_width], BF16)
+        laid["dom", 0] = stage[:, half_width // 2 : 3 * half_width // 2]
+        laid["ds", 1] = laid["qm", 1] = stage[:, 0:half_width]
+        laid["pw", 1] = stage[:, half_width : 2 * half_width]
 
         def quantize(name, h):
             cols = slice(h * HALF, (h + 1) * HALF)
@@ -100,7 +101,11 @@ def tile_attend_gat_pl_sig_c_kernel(tc, qT, cT, doT, rw, qm, dom, offs, out_0, o
         whole = slice(0, N)
         halves = (slice(0, HALF), slice(HALF, N))
         c_lanes = laid_c[:].rearrange("p (s j) -> p s j", j=PACK)
-        for j in range(PACK):
+        early_rows = sb("early_rows", [P, 2, N], BF16)
+        for j in range(2):
+            nc.scalar.activation(out=early_rows[:, j, :], in_=pool_planes[j][:].indirect(offsets[:]), func=ACT.Copy)
+        nc.vector.tensor_copy(out=c_lanes[:, :, 0:2], in_=early_rows[:].rearrange("p j s -> p s j"))
+        for j in range(2, PACK):
             nc.vector.tensor_copy(out=c_lanes[:, :, j], in_=pool_planes[j][:].indirect(offsets[:]))
         nc.vector.quantize_mx(out=codes["c"][:].bitcast(E4M3), scales=scales["c"][:], in_=laid_c[:])
         for name in ("q", "do"):
@@ -122,16 +127,18 @@ def tile_attend_gat_pl_sig_c_kernel(tc, qT, cT, doT, rw, qm, dom, offs, out_0, o
         for t in range(PACK):
             nc.scalar.activation(out=prob[t][:], in_=score[t][:], func=ACT.Sigmoid)
 
-        neg_pw = sb("neg_pw", [P, PACK, N], F32)
+        neg_pw = [sb("neg_pw%d" % h, [P, PACK, HALF], F32) for h in range(2)]
         neg_dq = sb("neg_dq", [P, PACK, N], F32)
-        nc.vector.tensor_scalar(
-            out=neg_pw[:, 0, :], in0=prob[0][:], scalar1=gate[:, 0:1], scalar2=-1.0, op0=ALU.mult, op1=ALU.mult
-        )
+        for h in range(2):
+            nc.vector.tensor_scalar(
+                out=neg_pw[h][:, 0, :], in0=prob[0][:, halves[h]], scalar1=gate[:, 0:1], scalar2=-1.0,
+                op0=ALU.mult, op1=ALU.mult,
+            )
         nc.gpsimd.tensor_scalar(out=neg_gate, in0=gate[:], scalar1=-1.0, scalar2=0.0, op0=ALU.mult, op1=ALU.add)
         for h in range(2):
             for t in range(1, PACK):
                 nc.gpsimd.tensor_scalar(
-                    out=neg_pw[:, t, halves[h]], in0=prob[t][:, halves[h]], scalar1=neg_gate[:, t : t + 1], scalar2=0.0,
+                    out=neg_pw[h][:, t, :], in0=prob[t][:, halves[h]], scalar1=neg_gate[:, t : t + 1], scalar2=0.0,
                     op0=ALU.mult, op1=ALU.add,
                 )
         for t in range(PACK):
@@ -145,75 +152,91 @@ def tile_attend_gat_pl_sig_c_kernel(tc, qT, cT, doT, rw, qm, dom, offs, out_0, o
         def woven(ap):
             return ap.rearrange("p (c i t) -> p c t i", i=4, t=PACK)
 
-        def weave_pw(h):
-            nc.scalar.activation(out=woven(laid["pw", h]), in_=runs(neg_pw[:, :, halves[h]]), func=ACT.Copy, scale=-1.0)
-
         def weave_ds(h):
             nc.vector.tensor_tensor(
-                out=woven(laid["ds", h]), in0=runs(neg_dq[:, :, halves[h]]), in1=runs(neg_pw[:, :, halves[h]]), op=ALU.mult
+                out=woven(laid["ds", h]), in0=runs(neg_dq[:, :, halves[h]]), in1=runs(neg_pw[h][:]), op=ALU.mult
             )
 
-        def product(j, index, slots, first, last):
-            grad = bank("grad%d" % index, index, slots.stop - slots.start)
-            mx(grad[:], first[0], j, first[1], slots, True, False)
-            mx(grad[:], last[0], j, last[1], slots, False, True)
-            return grad
+        def products(planes, h, first, last):
+            grads = {j: bank("grad%d%d" % (j, h), PACK * h + j, HALF) for j in planes}
+            for stat, mov in (first, last):
+                for j in planes:
+                    mx(grads[j][:], stat, j, mov, halves[h], stat == first[0], stat == last[0])
+            return grads
+
+        def evict(copy, grads, j, h):
+            copy(out=grad_sb[j, h][:], in_=grads[j][:])
 
         by_keys, by_values = ("qm", "ds"), ("dom", "pw")
         out_rows = out_0.rearrange("(p j) t -> j p t", j=PACK)
-        grad_sb = [sb("grad_sb%d" % j, [P, N], F32) for j in range(PACK)]
+        grad_sb = {(j, h): sb("grad_sb%d%d" % (j, h), [P, HALF], F32) for j in range(PACK) for h in range(2)}
 
         def scatter_half(j, h):
-            nc.scalar.activation(out=windows[j][:].indirect(list_halves[h]), in_=grad_sb[j][:, halves[h]], func=ACT.Copy)
+            window = windows[j][:].indirect(list_halves[h])
+            if h == 1 and j < 2:
+                nc.vector.tensor_copy(out=window, in_=grad_sb[j, h][:])
+            else:
+                nc.scalar.activation(out=window, in_=grad_sb[j, h][:], func=ACT.Copy)
 
         def store(j):
             nc.sync.dma_start(out=out_rows[j], in_=windows[j][:])
 
         deal(nc.scalar.copy, "qm", 0)
-        weave_pw(0)
-        deal(nc.scalar.copy, "dom", 0)
-        weave_ds(0)
-        quantize("qm", 0)
-        quantize("pw", 0)
-        weave_pw(1)
-        quantize("ds", 0)
-        quantize("dom", 0)
-        nc.scalar.copy(out=grad_sb[0][:, halves[0]], in_=product(0, 0, halves[0], by_keys, by_values)[:])
-        scatter_half(0, 0)
-        weave_ds(1)
-        quantize("pw", 1)
-        quantize("ds", 1)
-        nc.scalar.copy(out=grad_sb[0][:, halves[1]], in_=product(0, PACK, halves[1], by_values, by_keys)[:])
-        scatter_half(0, 1)
-        store(0)
-        grad1 = product(1, 1, whole, by_values, by_keys)
-        for name in ("qm", "dom"):
-            deal(nc.vector.tensor_copy, name, 1)
-        for name in ("qm", "dom"):
-            quantize(name, 1)
-        nc.vector.tensor_copy(out=grad_sb[1][:], in_=grad1[:])
-        nc.vector.tensor_copy(out=grad_sb[2][:], in_=product(2, 2, whole, by_keys, by_values)[:])
-        nc.vector.tensor_copy(out=windows[2][:].indirect(offsets[:]), in_=grad_sb[2][:])
-        store(2)
-        scatter_half(1, 0)
-        nc.scalar.copy(out=grad_sb[3][:], in_=product(3, 3, whole, by_keys, by_values)[:])
-        scatter_half(1, 1)
-        store(1)
+        nc.scalar.activation(out=woven(laid["pw", 0]), in_=runs(neg_pw[0][:]), func=ACT.Copy, scale=-1.0)
         for h in range(2):
-            scatter_half(3, h)
-        store(3)
+            deal(nc.scalar.copy, "dom", h)
+        weave_ds(0)
+        for name in ("qm", "ds", "pw", "dom"):
+            quantize(name, 0)
+        first_low = products((0, 1), 0, by_keys, by_values)
+        for j in (0, 1):
+            evict(nc.scalar.copy, first_low, j, 0)
+        for j in (0, 1):
+            scatter_half(j, 0)
+        weave_ds(1)
+        nc.vector.tensor_scalar(
+            out=woven(laid["pw", 1]), in0=runs(neg_pw[1][:]), scalar1=-1.0, scalar2=None, op0=ALU.mult
+        )
+        quantize("ds", 1)
+        quantize("pw", 1)
+        second_low = products((0, 1), 1, by_keys, by_values)
+        deal(nc.vector.tensor_copy, "qm", 1)
+        quantize("dom", 1)
+        quantize("qm", 1)
+        first_high = products((2, 3), 0, by_values, by_keys)
+        second_high = products((2, 3), 1, by_values, by_keys)
+        for j in (0, 1):
+            evict(nc.vector.tensor_copy, second_low, j, 1)
+        for j in (0, 1):
+            scatter_half(j, 1)
+            store(j)
+        for j in (2, 3):
+            evict(nc.scalar.copy, first_high, j, 0)
+        for j in (2, 3):
+            scatter_half(j, 0)
+        for j in (2, 3):
+            evict(nc.scalar.copy, second_high, j, 1)
+        for j in (2, 3):
+            scatter_half(j, 1)
+            store(j)
 
-        pairs = sb("pairs", [P, 2, T * 2], BF16, "codes_pw")
+        pairs = sb("pairs", [P, 2, T * 2], BF16)
+
+        def pair_words(lo, hi):
+            return pairs[:, :, 2 * lo : 2 * hi]
 
         def pair_lanes(j, lo, hi):
-            return pairs[:, j // 2, 2 * lo : 2 * hi].rearrange("p (t e) -> p t e", e=2)
+            return pair_words(lo, hi)[:, j // 2, :].rearrange("p (t e) -> p t e", e=2)
 
-        nc.vector.tensor_copy(out=pair_lanes(0, 0, T)[:, :, 0], in_=windows[0][:])
-        nc.vector.tensor_copy(out=pair_lanes(2, 0, SPLIT)[:, :, 0], in_=windows[2][:, 0:SPLIT])
+        def round_lane(copy, j, lo, hi):
+            copy(out=pair_lanes(j, lo, hi)[:, :, j % 2], in_=windows[j][:, lo:hi])
+
+        round_lane(nc.vector.tensor_copy, 0, 0, T)
         nc.vector.tensor_copy(
             out=pair_lanes(2, SPLIT, T), in_=windows[2][:, SPLIT:T].unsqueeze(2).to_broadcast([P, T - SPLIT, 2])
         )
-        nc.vector.tensor_copy(out=pair_lanes(1, 0, T)[:, :, 1], in_=windows[1][:])
+        round_lane(nc.vector.tensor_copy, 1, 0, T)
+        round_lane(nc.vector.tensor_copy, 2, 0, SPLIT)
 
         chunks = VECTOR_CHUNKS + SCALAR_CHUNKS
         out_laid = {c: sb("out_laid%d" % c[0], [P, (c[1] - c[0]) * PACK], BF16) for c in chunks}
@@ -222,13 +245,13 @@ def tile_attend_gat_pl_sig_c_kernel(tc, qT, cT, doT, rw, qm, dom, offs, out_0, o
         words_dram = out_1[0].rearrange("p t l -> p (t l)").bitcast(I32)
 
         def weave_pairs(copy, c):
-            src = pairs[:, :, 2 * c[0] : 2 * c[1]].bitcast(F32).rearrange("p u t -> p t u")
+            src = pair_words(*c).bitcast(F32).rearrange("p u t -> p t u")
             copy(out=out_laid[c][:].bitcast(F32).rearrange("p (t u) -> p t u", u=2), in_=src)
 
         def quantize_out(c):
             lo = c[0]
             for hi in range(c[0] + P, c[1] + 1, P):
-                if hi % 256 == 0 or hi == c[1]:
+                if hi == c[1]:
                     quarter, col = divmod(lo, QUARTER)
                     nc.vector.quantize_mx(
                         out=out_codes[:, lo:hi].bitcast(E4M3),
@@ -238,9 +261,9 @@ def tile_attend_gat_pl_sig_c_kernel(tc, qT, cT, doT, rw, qm, dom, offs, out_0, o
                     lo = hi
 
         for c in VECTOR_CHUNKS:
-            nc.vector.tensor_copy(out=pair_lanes(3, *c)[:, :, 1], in_=windows[3][:, c[0] : c[1]])
+            round_lane(nc.vector.tensor_copy, 3, *c)
         for lo, hi in ((SPLIT, SCALAR_CHUNKS[0][1]), (SCALAR_CHUNKS[0][1], T)):
-            nc.scalar.copy(out=pair_lanes(3, lo, hi)[:, :, 1], in_=windows[3][:, lo:hi])
+            round_lane(nc.scalar.copy, 3, lo, hi)
         for c in VECTOR_CHUNKS:
             weave_pairs(nc.vector.tensor_copy, c)
         for c in SCALAR_CHUNKS:

@@ -20,9 +20,9 @@ P = 128
 PACK = 4
 HALF = N // 2
 QUARTER = T // PACK
-SPLIT = 768
-VECTOR_CHUNKS = ((0, 512), (512, SPLIT))
-SCALAR_CHUNKS = ((SPLIT, 1024), (1024, 1536), (1536, 1792), (1792, 1920), (1920, T))
+SPLIT = 1152
+VECTOR_CHUNKS = ((0, 512), (512, 1024), (1024, SPLIT))
+SCALAR_CHUNKS = ((SPLIT, 1280), (1280, 1536), (1536, 1792), (1792, 1920), (1920, T))
 STORE_ENDS = (512, 1024, 1536, T)
 FORMATS = {"c": E4M3, "q": E4M3, "do": E5M2, "qm": E4M3, "dom": E5M2, "ds": E5M2, "pw": E4M3}
 
@@ -262,7 +262,7 @@ def tile_attend_gat_pl_sig_c_kernel(tc, qT, cT, doT, rw, qm, dom, offs, out_0, o
 
         for c in VECTOR_CHUNKS:
             round_lane(nc.vector.tensor_copy, 3, *c)
-        for lo, hi in ((SPLIT, SCALAR_CHUNKS[0][1]), (SCALAR_CHUNKS[0][1], T)):
+        for lo, hi in ((SPLIT, 1536), (1536, T)):
             round_lane(nc.scalar.copy, 3, lo, hi)
         for c in VECTOR_CHUNKS:
             weave_pairs(nc.vector.tensor_copy, c)

@@ -101,11 +101,7 @@ def tile_attend_gat_pl_sig_c_kernel(tc, qT, cT, doT, rw, qm, dom, offs, out_0, o
         whole = slice(0, N)
         halves = (slice(0, HALF), slice(HALF, N))
         c_lanes = laid_c[:].rearrange("p (s j) -> p s j", j=PACK)
-        early_rows = sb("early_rows", [P, 2, N], BF16)
-        for j in range(2):
-            nc.scalar.activation(out=early_rows[:, j, :], in_=pool_planes[j][:].indirect(offsets[:]), func=ACT.Copy)
-        nc.vector.tensor_copy(out=c_lanes[:, :, 0:2], in_=early_rows[:].rearrange("p j s -> p s j"))
-        for j in range(2, PACK):
+        for j in range(PACK):
             nc.vector.tensor_copy(out=c_lanes[:, :, j], in_=pool_planes[j][:].indirect(offsets[:]))
         nc.vector.quantize_mx(out=codes["c"][:].bitcast(E4M3), scales=scales["c"][:], in_=laid_c[:])
         for name in ("q", "do"):

@@ -20,9 +20,9 @@ P = 128
 PACK = 4
 HALF = N // 2
 QUARTER = T // PACK
-SPLIT = 1152
-VECTOR_CHUNKS = ((0, 512), (512, 1024), (1024, SPLIT))
-SCALAR_CHUNKS = ((SPLIT, 1280), (1280, 1536), (1536, 1792), (1792, 1920), (1920, T))
+SPLIT = 1024
+VECTOR_CHUNKS = ((0, 512), (512, SPLIT))
+SCALAR_CHUNKS = ((SPLIT, 1536), (1536, 1792), (1792, 1920), (1920, T))
 STORE_ENDS = (512, 1024, 1536, T)
 FORMATS = {"c": E4M3, "q": E4M3, "do": E5M2, "qm": E4M3, "dom": E5M2, "ds": E5M2, "pw": E4M3}
 
@@ -65,11 +65,13 @@ def tile_attend_gat_pl_sig_c_kernel(tc, qT, cT, doT, rw, qm, dom, offs, out_0, o
         scales = {name: sb("scales_" + name, [P, 512], U8) for name in FORMATS}
         half_width = HALF * PACK
         laid_c = sb("laid_c", [P, N * PACK], BF16)
-        own_bytes = (("q", 0), ("q", 1), ("do", 0), ("qm", 0), ("ds", 0), ("pw", 0), ("dom", 1))
+        own_bytes = (("q", 0), ("q", 1), ("do", 0), ("ds", 0), ("pw", 0), ("dom", 1))
         laid = {key: sb("laid_%s%d" % key, [P, half_width], BF16)[:] for key in own_bytes}
-        late_do = sb("late_do", [P, HALF * 2], F32)
-        laid["do", 1] = late_do[:].bitcast(BF16)
-        neg_gate = late_do[:, 0:PACK]
+        neg_pw_flat = sb("neg_pw", [P, PACK * N], F32)
+        neg_pw = neg_pw_flat[:].rearrange("p (h t s) -> p h t s", h=2, t=PACK)
+        straddle = neg_pw_flat[:, 3 * HALF // 2 : 11 * HALF // 2].bitcast(BF16).rearrange("p (t w) -> p t w", t=2)
+        late_do = straddle[:, :, 0 : P * PACK]
+        laid["qm", 0] = neg_pw_flat[:, 11 * HALF // 2 : 15 * HALF // 2].bitcast(BF16)
         stage = sb("stage", [P, 2 * half_width], BF16)
         laid["dom", 0] = stage[:, half_width // 2 : 3 * half_width // 2]
         laid["ds", 1] = laid["qm", 1] = stage[:, 0:half_width]
@@ -104,11 +106,16 @@ def tile_attend_gat_pl_sig_c_kernel(tc, qT, cT, doT, rw, qm, dom, offs, out_0, o
         for j in range(PACK):
             nc.vector.tensor_copy(out=c_lanes[:, :, j], in_=pool_planes[j][:].indirect(offsets[:]))
         nc.vector.quantize_mx(out=codes["c"][:].bitcast(E4M3), scales=scales["c"][:], in_=laid_c[:])
-        for name in ("q", "do"):
-            for h in range(2):
-                deal(nc.vector.tensor_copy, name, h)
-            for h in range(2):
-                quantize(name, h)
+        for h in range(2):
+            deal(nc.vector.tensor_copy, "q", h)
+        for h in range(2):
+            quantize("q", h)
+        deal(nc.vector.tensor_copy, "do", 0)
+        nc.vector.tensor_copy(
+            out=late_do.rearrange("p t (m j) -> p m j t", j=PACK),
+            in_=raw["do"][:].rearrange("p j (m t) -> p m j t", t=PACK)[:, :, :, 2:4],
+        )
+        quantize("do", 0)
 
         def bank(name, index, width):
             return psum.tile([P, width], F32, name=name, tag="bank%d" % index)
@@ -119,24 +126,23 @@ def tile_attend_gat_pl_sig_c_kernel(tc, qT, cT, doT, rw, qm, dom, offs, out_0, o
         for t in range(PACK):
             mx(score[t][:], "q", t, "c", whole, True, True)
         for t in range(PACK):
-            mx(dprob[t][:], "do", t, "c", whole, True, True)
-        for t in range(PACK):
             nc.scalar.activation(out=prob[t][:], in_=score[t][:], func=ACT.Sigmoid)
 
-        neg_pw = [sb("neg_pw%d" % h, [P, PACK, HALF], F32) for h in range(2)]
-        neg_dq = sb("neg_dq", [P, PACK, N], F32)
-        for h in range(2):
-            nc.vector.tensor_scalar(
-                out=neg_pw[h][:, 0, :], in0=prob[0][:, halves[h]], scalar1=gate[:, 0:1], scalar2=-1.0,
-                op0=ALU.mult, op1=ALU.mult,
+        def gate_product(engine, t, h):
+            engine.tensor_scalar(
+                out=neg_pw[:, h, t, :], in0=prob[t][:, halves[h]],
+                scalar1=gate[:, t : t + 1], scalar2=-1.0, op0=ALU.mult, op1=ALU.mult,
             )
-        nc.gpsimd.tensor_scalar(out=neg_gate, in0=gate[:], scalar1=-1.0, scalar2=0.0, op0=ALU.mult, op1=ALU.add)
-        for h in range(2):
-            for t in range(1, PACK):
-                nc.gpsimd.tensor_scalar(
-                    out=neg_pw[h][:, t, :], in0=prob[t][:, halves[h]], scalar1=neg_gate[:, t : t + 1], scalar2=0.0,
-                    op0=ALU.mult, op1=ALU.add,
-                )
+
+        neg_dq = sb("neg_dq", [P, PACK, N], F32)
+        gate_product(nc.vector, 0, 0)
+        for t in (2, 3):
+            cols = slice(P * t, P * (t + 1))
+            nc.vector.quantize_mx(out=codes["do"][:, cols].bitcast(E5M2), scales=scales["do"][:, cols], in_=late_do[:, t - 2, :])
+        for t in range(PACK):
+            mx(dprob[t][:], "do", t, "c", whole, True, True)
+        for t, h in ((1, 0), (2, 0), (3, 0), (0, 1)):
+            gate_product(nc.gpsimd, t, h)
         for t in range(PACK):
             nc.vector.scalar_tensor_tensor(
                 out=neg_dq[:, t, :], in0=prob[t][:], scalar=1.0, in1=dprob[t][:], op0=ALU.subtract, op1=ALU.mult
@@ -150,7 +156,7 @@ def tile_attend_gat_pl_sig_c_kernel(tc, qT, cT, doT, rw, qm, dom, offs, out_0, o
 
         def weave_ds(h):
             nc.vector.tensor_tensor(
-                out=woven(laid["ds", h]), in0=runs(neg_dq[:, :, halves[h]]), in1=runs(neg_pw[h][:]), op=ALU.mult
+                out=woven(laid["ds", h]), in0=runs(neg_dq[:, :, halves[h]]), in1=runs(neg_pw[:, h]), op=ALU.mult
             )
 
         def products(planes, h, first, last):
@@ -178,12 +184,14 @@ def tile_attend_gat_pl_sig_c_kernel(tc, qT, cT, doT, rw, qm, dom, offs, out_0, o
             nc.sync.dma_start(out=out_rows[j], in_=windows[j][:])
 
         deal(nc.scalar.copy, "qm", 0)
-        nc.scalar.activation(out=woven(laid["pw", 0]), in_=runs(neg_pw[0][:]), func=ACT.Copy, scale=-1.0)
+        nc.scalar.activation(out=woven(laid["pw", 0]), in_=runs(neg_pw[:, 0]), func=ACT.Copy, scale=-1.0)
         for h in range(2):
             deal(nc.scalar.copy, "dom", h)
         weave_ds(0)
         for name in ("qm", "ds", "pw", "dom"):
             quantize(name, 0)
+        for t in (1, 2, 3):
+            gate_product(nc.vector, t, 1)
         first_low = products((0, 1), 0, by_keys, by_values)
         for j in (0, 1):
             evict(nc.scalar.copy, first_low, j, 0)
@@ -191,7 +199,7 @@ def tile_attend_gat_pl_sig_c_kernel(tc, qT, cT, doT, rw, qm, dom, offs, out_0, o
             scatter_half(j, 0)
         weave_ds(1)
         nc.vector.tensor_scalar(
-            out=woven(laid["pw", 1]), in0=runs(neg_pw[1][:]), scalar1=-1.0, scalar2=None, op0=ALU.mult
+            out=woven(laid["pw", 1]), in0=runs(neg_pw[:, 1]), scalar1=-1.0, scalar2=None, op0=ALU.mult
         )
         quantize("ds", 1)
         quantize("pw", 1)
@@ -247,7 +255,7 @@ def tile_attend_gat_pl_sig_c_kernel(tc, qT, cT, doT, rw, qm, dom, offs, out_0, o
         def quantize_out(c):
             lo = c[0]
             for hi in range(c[0] + P, c[1] + 1, P):
-                if hi == c[1]:
+                if hi % 256 == 0 or hi == c[1]:
                     quarter, col = divmod(lo, QUARTER)
                     nc.vector.quantize_mx(
                         out=out_codes[:, lo:hi].bitcast(E4M3),

@@ -1,6 +1,7 @@
 from contextlib import ExitStack
 
 import concourse.mybir as mybir
+from concourse.masks import make_identity
 
 N, T, D, R = 512, 2048, 512, 512
 FLOPS = 4 * 2 * R * N * D
@@ -23,7 +24,8 @@ QUARTER = T // PACK
 SPLIT = 1024
 VECTOR_CHUNKS = ((0, 512), (512, SPLIT))
 SCALAR_CHUNKS = ((SPLIT, 1536), (1536, 1792), (1792, 1920), (1920, T))
-STORE_ENDS = (512, 1024, 1536, T)
+HANDED = 1280
+STORE_STARTS = {768: 0, 1536: 768, T: 1536}
 FORMATS = {"c": E4M3, "q": E4M3, "do": E5M2, "qm": E4M3, "dom": E5M2, "ds": E5M2, "pw": E4M3}
 
 
@@ -47,15 +49,24 @@ def tile_attend_gat_pl_sig_c_kernel(tc, qT, cT, doT, rw, qm, dom, offs, out_0, o
         def load(name, src):
             nc.sync.dma_start(out=raw[name][:], in_=src[0].rearrange("(p j) w -> p j w", j=PACK))
 
+        gate_row = sb("gate_row", [P, R], F32)
+        nc.vector.memset(gate_row[:], 0.0)
         for j in range(PACK):
             nc.sync.dma_start(out=pool_planes[j][:], in_=c_rows[j])
             if j == 0:
                 nc.sync.dma_start(offsets[:], offs)
+                nc.sync.dma_start(out=gate_row[0:1, :], in_=rw[0].rearrange("r o -> o r"))
         load("q", qT)
         load("do", doT)
-        nc.sync.dma_start(out=gate[:], in_=rw[0].rearrange("(p t) o -> p (t o)", t=PACK))
         load("qm", qm)
         load("dom", dom)
+
+        identity = sb("identity", [P, P], F32)
+        make_identity(nc, identity[:])
+        turned = psum.tile([P, PACK, P], F32, name="turned", tag="bank7")
+        for t in range(PACK):
+            nc.tensor.transpose(turned[:, t, :], gate_row[:, t:R:PACK], identity[:])
+        nc.vector.tensor_copy(out=gate[:], in_=turned[:, :, 0])
 
         windows = [sb("window%d" % j, [P, T], F32) for j in range(PACK)]
         for j in range(PACK):
@@ -77,16 +88,17 @@ def tile_attend_gat_pl_sig_c_kernel(tc, qT, cT, doT, rw, qm, dom, offs, out_0, o
         laid["ds", 1] = laid["qm", 1] = stage[:, 0:half_width]
         laid["pw", 1] = stage[:, half_width : 2 * half_width]
 
-        def quantize(name, h):
-            cols = slice(h * HALF, (h + 1) * HALF)
+        def quantize(name, h, first=0, count=2):
+            cols = slice(h * HALF + P * first, h * HALF + P * (first + count))
             nc.vector.quantize_mx(
-                out=codes[name][:, cols].bitcast(FORMATS[name]), scales=scales[name][:, cols], in_=laid[name, h]
+                out=codes[name][:, cols].bitcast(FORMATS[name]), scales=scales[name][:, cols],
+                in_=laid[name, h][:, PACK * P * first : PACK * P * (first + count)],
             )
 
-        def deal(copy, name, h):
+        def deal(copy, name, h, places=slice(0, P)):
             dst = laid[name, h].rearrange("p (t m j) -> p m j t", t=2, j=PACK)
             src = raw[name][:].rearrange("p j (m t) -> p m j t", t=PACK)
-            copy(out=dst, in_=src[:, :, :, 2 * h : 2 * h + 2])
+            copy(out=dst[:, places], in_=src[:, places, :, 2 * h : 2 * h + 2])
 
         def mx(out, stat, tile_index, mov, slots, start, stop):
             cols = slice(P * tile_index, P * (tile_index + 1))
@@ -106,10 +118,11 @@ def tile_attend_gat_pl_sig_c_kernel(tc, qT, cT, doT, rw, qm, dom, offs, out_0, o
         for j in range(PACK):
             nc.vector.tensor_copy(out=c_lanes[:, :, j], in_=pool_planes[j][:].indirect(offsets[:]))
         nc.vector.quantize_mx(out=codes["c"][:].bitcast(E4M3), scales=scales["c"][:], in_=laid_c[:])
-        for h in range(2):
-            deal(nc.vector.tensor_copy, "q", h)
-        for h in range(2):
-            quantize("q", h)
+        deal(nc.vector.tensor_copy, "q", 0)
+        for t in range(2):
+            deal(nc.vector.tensor_copy, "q", 1, slice(t * P // 2, (t + 1) * P // 2))
+            quantize("q", 0, t, 1)
+        quantize("q", 1)
         deal(nc.vector.tensor_copy, "do", 0)
         nc.vector.tensor_copy(
             out=late_do.rearrange("p t (m j) -> p m j t", j=PACK),
@@ -235,11 +248,12 @@ def tile_attend_gat_pl_sig_c_kernel(tc, qT, cT, doT, rw, qm, dom, offs, out_0, o
         def round_lane(copy, j, lo, hi):
             copy(out=pair_lanes(j, lo, hi)[:, :, j % 2], in_=windows[j][:, lo:hi])
 
-        round_lane(nc.vector.tensor_copy, 0, 0, T)
+        for j in (0, 1):
+            round_lane(nc.vector.tensor_copy, j, 0, T)
         nc.vector.tensor_copy(
-            out=pair_lanes(2, SPLIT, T), in_=windows[2][:, SPLIT:T].unsqueeze(2).to_broadcast([P, T - SPLIT, 2])
+            out=pair_lanes(2, HANDED, T), in_=windows[2][:, HANDED:T].unsqueeze(2).to_broadcast([P, T - HANDED, 2])
         )
-        round_lane(nc.vector.tensor_copy, 1, 0, T)
+        round_lane(nc.scalar.copy, 2, SPLIT, HANDED)
         round_lane(nc.vector.tensor_copy, 2, 0, SPLIT)
 
         chunks = VECTOR_CHUNKS + SCALAR_CHUNKS
@@ -262,6 +276,9 @@ def tile_attend_gat_pl_sig_c_kernel(tc, qT, cT, doT, rw, qm, dom, offs, out_0, o
                         scales=out_scales[4 * quarter : P, col : col + hi - lo],
                         in_=out_laid[c][:, PACK * (lo - c[0]) : PACK * (hi - c[0])],
                     )
+                    if hi in STORE_STARTS:
+                        first = STORE_STARTS[hi]
+                        nc.sync.dma_start(out=words_dram[:, first:hi], in_=out_codes[:, first:hi].bitcast(I32))
                     lo = hi
 
         for c in VECTOR_CHUNKS:
@@ -272,12 +289,8 @@ def tile_attend_gat_pl_sig_c_kernel(tc, qT, cT, doT, rw, qm, dom, offs, out_0, o
             weave_pairs(nc.vector.tensor_copy, c)
         for c in SCALAR_CHUNKS:
             weave_pairs(nc.scalar.copy, c)
-        stored = 0
         for c in chunks:
             quantize_out(c)
-            if c[1] in STORE_ENDS:
-                nc.sync.dma_start(out=words_dram[:, stored : c[1]], in_=out_codes[:, stored : c[1]].bitcast(I32))
-                stored = c[1]
         for queue, quad in zip((nc.scalar, nc.scalar, nc.sync, nc.scalar), (0, 2, 1, 3)):
             queue.dma_start(
                 out=out_2[0, 4 * quad : 4 * quad + 4, :].bitcast(I32).rearrange("f (u c) -> u f c", u=PACK),

@@ -25,6 +25,8 @@ SPLIT = 1024
 VECTOR_CHUNKS = ((0, 512), (512, SPLIT))
 SCALAR_CHUNKS = ((SPLIT, 1536), (1536, 1792), (1792, 1920), (1920, T))
 HANDED = 1280
+BESIDE = 1024
+HANDOVER = 16
 STORE_STARTS = {768: 0, 1536: 768, T: 1536}
 FORMATS = {"c": E4M3, "q": E4M3, "do": E5M2, "qm": E4M3, "dom": E5M2, "ds": E5M2, "pw": E4M3}
 
@@ -44,7 +46,7 @@ def tile_attend_gat_pl_sig_c_kernel(tc, qT, cT, doT, rw, qm, dom, offs, out_0, o
         pool_planes = [sb("pool%d" % j, [P, T], F32) for j in range(PACK)]
         c_rows = cT.rearrange("(p j) t -> j p t", j=PACK)
         raw = {name: sb("raw_" + name, [P, PACK, 512], F32) for name in ("q", "do", "qm", "dom")}
-        gate = sb("gate", [P, PACK], F32)
+        neg_gate = sb("neg_gate", [P, PACK], F32)
 
         def load(name, src):
             nc.sync.dma_start(out=raw[name][:], in_=src[0].rearrange("(p j) w -> p j w", j=PACK))
@@ -66,7 +68,7 @@ def tile_attend_gat_pl_sig_c_kernel(tc, qT, cT, doT, rw, qm, dom, offs, out_0, o
         turned = psum.tile([P, PACK, P], F32, name="turned", tag="bank7")
         for t in range(PACK):
             nc.tensor.transpose(turned[:, t, :], gate_row[:, t:R:PACK], identity[:])
-        nc.vector.tensor_copy(out=gate[:], in_=turned[:, :, 0])
+        nc.vector.tensor_scalar(out=neg_gate[:], in0=turned[:, :, 0], scalar1=-1.0, scalar2=None, op0=ALU.mult)
 
         windows = [sb("window%d" % j, [P, T], F32) for j in range(PACK)]
         for j in range(PACK):
@@ -76,15 +78,14 @@ def tile_attend_gat_pl_sig_c_kernel(tc, qT, cT, doT, rw, qm, dom, offs, out_0, o
         scales = {name: sb("scales_" + name, [P, 512], U8) for name in FORMATS}
         half_width = HALF * PACK
         laid_c = sb("laid_c", [P, N * PACK], BF16)
-        own_bytes = (("q", 0), ("q", 1), ("do", 0), ("ds", 0), ("pw", 0), ("dom", 1))
+        own_bytes = (("q", 0), ("q", 1), ("do", 0), ("ds", 0), ("pw", 0), ("qm", 0), ("dom", 1))
         laid = {key: sb("laid_%s%d" % key, [P, half_width], BF16)[:] for key in own_bytes}
         neg_pw_flat = sb("neg_pw", [P, PACK * N], F32)
         neg_pw = neg_pw_flat[:].rearrange("p (h t s) -> p h t s", h=2, t=PACK)
-        straddle = neg_pw_flat[:, 3 * HALF // 2 : 11 * HALF // 2].bitcast(BF16).rearrange("p (t w) -> p t w", t=2)
-        late_do = straddle[:, :, 0 : P * PACK]
-        laid["qm", 0] = neg_pw_flat[:, 11 * HALF // 2 : 15 * HALF // 2].bitcast(BF16)
+        straddle = neg_pw_flat[:, 4 * HALF : 8 * HALF].bitcast(BF16).rearrange("p (t w) -> p t w", t=2)
+        late_do = straddle[:, :, HALF : HALF + P * PACK]
         stage = sb("stage", [P, 2 * half_width], BF16)
-        laid["dom", 0] = stage[:, half_width // 2 : 3 * half_width // 2]
+        laid["dom", 0] = stage[:, 3 * half_width // 4 : 7 * half_width // 4]
         laid["ds", 1] = laid["qm", 1] = stage[:, 0:half_width]
         laid["pw", 1] = stage[:, half_width : 2 * half_width]
 
@@ -115,9 +116,15 @@ def tile_attend_gat_pl_sig_c_kernel(tc, qT, cT, doT, rw, qm, dom, offs, out_0, o
         whole = slice(0, N)
         halves = (slice(0, HALF), slice(HALF, N))
         c_lanes = laid_c[:].rearrange("p (s j) -> p s j", j=PACK)
-        for j in range(PACK):
+        for j in range(PACK - 1):
             nc.vector.tensor_copy(out=c_lanes[:, :, j], in_=pool_planes[j][:].indirect(offsets[:]))
-        nc.vector.quantize_mx(out=codes["c"][:].bitcast(E4M3), scales=scales["c"][:], in_=laid_c[:])
+        for h in range(2):
+            nc.vector.tensor_copy(out=c_lanes[:, halves[h], PACK - 1], in_=pool_planes[PACK - 1][:].indirect(list_halves[h]))
+        for h in range(2):
+            nc.vector.quantize_mx(
+                out=codes["c"][:, halves[h]].bitcast(E4M3), scales=scales["c"][:, halves[h]],
+                in_=laid_c[:, h * half_width : (h + 1) * half_width],
+            )
         deal(nc.vector.tensor_copy, "q", 0)
         for t in range(2):
             deal(nc.vector.tensor_copy, "q", 1, slice(t * P // 2, (t + 1) * P // 2))
@@ -142,10 +149,14 @@ def tile_attend_gat_pl_sig_c_kernel(tc, qT, cT, doT, rw, qm, dom, offs, out_0, o
             nc.scalar.activation(out=prob[t][:], in_=score[t][:], func=ACT.Sigmoid)
 
         def gate_product(engine, t, h):
-            engine.tensor_scalar(
-                out=neg_pw[:, h, t, :], in0=prob[t][:, halves[h]],
-                scalar1=gate[:, t : t + 1], scalar2=-1.0, op0=ALU.mult, op1=ALU.mult,
-            )
+            out, in_, factor = neg_pw[:, h, t, :], prob[t][:, halves[h]], neg_gate[:, t : t + 1]
+            if engine is nc.scalar:
+                engine.activation(out=out, in_=in_, func=ACT.Copy, scale=factor)
+            else:
+                engine.tensor_scalar(out=out, in0=in_, scalar1=factor, scalar2=0.0, op0=ALU.mult, op1=ALU.add)
+
+        def gpsimd_round(out, in_):
+            nc.gpsimd.tensor_scalar(out=out, in0=in_, scalar1=1.0, scalar2=0.0, op0=ALU.mult, op1=ALU.add)
 
         neg_dq = sb("neg_dq", [P, PACK, N], F32)
         gate_product(nc.vector, 0, 0)
@@ -154,8 +165,10 @@ def tile_attend_gat_pl_sig_c_kernel(tc, qT, cT, doT, rw, qm, dom, offs, out_0, o
             nc.vector.quantize_mx(out=codes["do"][:, cols].bitcast(E5M2), scales=scales["do"][:, cols], in_=late_do[:, t - 2, :])
         for t in range(PACK):
             mx(dprob[t][:], "do", t, "c", whole, True, True)
-        for t, h in ((1, 0), (2, 0), (3, 0), (0, 1)):
-            gate_product(nc.gpsimd, t, h)
+        for t in (1, 2, 3):
+            gate_product(nc.scalar, t, 0)
+        for t in range(PACK):
+            gate_product(nc.gpsimd, t, 1)
         for t in range(PACK):
             nc.vector.scalar_tensor_tensor(
                 out=neg_dq[:, t, :], in0=prob[t][:], scalar=1.0, in1=dprob[t][:], op0=ALU.subtract, op1=ALU.mult
@@ -201,10 +214,10 @@ def tile_attend_gat_pl_sig_c_kernel(tc, qT, cT, doT, rw, qm, dom, offs, out_0, o
         for h in range(2):
             deal(nc.scalar.copy, "dom", h)
         weave_ds(0)
-        for name in ("qm", "ds", "pw", "dom"):
+        for name in ("qm", "ds", "pw"):
             quantize(name, 0)
-        for t in (1, 2, 3):
-            gate_product(nc.vector, t, 1)
+        for t in range(2):
+            quantize("dom", 0, t, 1)
         first_low = products((0, 1), 0, by_keys, by_values)
         for j in (0, 1):
             evict(nc.scalar.copy, first_low, j, 0)
@@ -224,20 +237,21 @@ def tile_attend_gat_pl_sig_c_kernel(tc, qT, cT, doT, rw, qm, dom, offs, out_0, o
         second_high = products((2, 3), 1, by_values, by_keys)
         for j in (0, 1):
             evict(nc.vector.tensor_copy, second_low, j, 1)
-        for j in (0, 1):
-            scatter_half(j, 1)
-            store(j)
+        scatter_half(0, 1)
+        store(0)
+        for j in (2, 3):
+            evict(nc.vector.tensor_copy, second_high, j, 1)
+        scatter_half(1, 1)
+        store(1)
         for j in (2, 3):
             evict(nc.scalar.copy, first_high, j, 0)
         for j in (2, 3):
             scatter_half(j, 0)
         for j in (2, 3):
-            evict(nc.scalar.copy, second_high, j, 1)
-        for j in (2, 3):
             scatter_half(j, 1)
             store(j)
 
-        pairs = sb("pairs", [P, 2, T * 2], BF16)
+        pairs = sb("pairs", [P, 2, T * 2], BF16, tag="codes_qm")
 
         def pair_words(lo, hi):
             return pairs[:, :, 2 * lo : 2 * hi]
@@ -248,13 +262,22 @@ def tile_attend_gat_pl_sig_c_kernel(tc, qT, cT, doT, rw, qm, dom, offs, out_0, o
         def round_lane(copy, j, lo, hi):
             copy(out=pair_lanes(j, lo, hi)[:, :, j % 2], in_=windows[j][:, lo:hi])
 
-        for j in (0, 1):
-            round_lane(nc.vector.tensor_copy, j, 0, T)
-        nc.vector.tensor_copy(
-            out=pair_lanes(2, HANDED, T), in_=windows[2][:, HANDED:T].unsqueeze(2).to_broadcast([P, T - HANDED, 2])
+        round_lane(gpsimd_round, 0, BESIDE, T - HANDOVER)
+        gpsimd_round(
+            out=pair_lanes(0, T - HANDOVER, T),
+            in_=windows[0][:, T - HANDOVER : T].unsqueeze(2).to_broadcast([P, HANDOVER, 2]),
         )
+        round_lane(nc.vector.tensor_copy, 0, 0, BESIDE)
+        round_lane(nc.vector.tensor_copy, 1, 0, BESIDE)
+        round_lane(nc.vector.tensor_copy, 1, BESIDE, T)
+        round_lane(nc.vector.tensor_copy, 2, HANDED, T)
         round_lane(nc.scalar.copy, 2, SPLIT, HANDED)
-        round_lane(nc.vector.tensor_copy, 2, 0, SPLIT)
+        round_lane(nc.vector.tensor_copy, 2, *VECTOR_CHUNKS[0])
+        lo, hi = 1536 - HANDOVER // 2, 1536 + HANDOVER // 2
+        nc.vector.tensor_copy(
+            out=pair_lanes(2, lo, hi), in_=windows[2][:, lo:hi].unsqueeze(2).to_broadcast([P, HANDOVER, 2])
+        )
+        round_lane(nc.vector.tensor_copy, 2, *VECTOR_CHUNKS[1])
 
         chunks = VECTOR_CHUNKS + SCALAR_CHUNKS
         out_laid = {c: sb("out_laid%d" % c[0], [P, (c[1] - c[0]) * PACK], BF16) for c in chunks}

from contextlib import ExitStack

import concourse.mybir as mybir
from concourse.masks import make_identity

N, T, D, R = 512, 2048, 512, 512
FLOPS = 4 * 2 * R * N * D

F32 = mybir.dt.float32
BF16 = mybir.dt.bfloat16
U32 = mybir.dt.uint32
I32 = mybir.dt.int32
U16 = mybir.dt.uint16
U8 = mybir.dt.uint8
E4M3 = mybir.dt.float8_e4m3fn_x4
E5M2 = mybir.dt.float8_e5m2_x4
ACT = mybir.ActivationFunctionType
ALU = mybir.AluOpType

P = 128
PACK = 4
HALF = N // 2
QUARTER = T // PACK
SPLIT = 1024
VECTOR_CHUNKS = ((0, 512), (512, SPLIT))
SCALAR_CHUNKS = ((SPLIT, 1536), (1536, 1792), (1792, 1920), (1920, T))
HANDED = 1280
BESIDE = 1024
HANDOVER = 16
STORE_STARTS = {768: 0, 1536: 768, T: 1536}
FORMATS = {"c": E4M3, "q": E4M3, "do": E5M2, "qm": E4M3, "dom": E5M2, "ds": E5M2, "pw": E4M3}


def tile_attend_gat_pl_sig_c_kernel(tc, qT, cT, doT, rw, qm, dom, offs, out_0, out_1, out_2):
    nc = tc.nc
    with ExitStack() as ctx:
        keep = ctx.enter_context(tc.tile_pool(name="keep", bufs=1))
        psum = ctx.enter_context(tc.psum_pool(name="psum", bufs=1))

        def sb(name, shape, dtype, tag=None):
            return keep.tile(shape, dtype, name=name, tag=tag or name, align_bytes=64)

        offsets = keep.tile([P, N // 16], U16, name="offsets")
        list_halves = [offsets[:, h * HALF // 16 : (h + 1) * HALF // 16] for h in range(2)]

        pool_planes = [sb("pool%d" % j, [P, T], F32) for j in range(PACK)]
        c_rows = cT.rearrange("(p j) t -> j p t", j=PACK)
        raw = {name: sb("raw_" + name, [P, PACK, 512], F32) for name in ("q", "do", "qm", "dom")}
        neg_gate = sb("neg_gate", [P, PACK], F32)

        def load(name, src):
            nc.sync.dma_start(out=raw[name][:], in_=src[0].rearrange("(p j) w -> p j w", j=PACK))

        gate_row = sb("gate_row", [P, R], F32)
        nc.vector.memset(gate_row[:], 0.0)
        for j in range(PACK):
            nc.sync.dma_start(out=pool_planes[j][:], in_=c_rows[j])
            if j == 0:
                nc.sync.dma_start(offsets[:], offs)
                nc.sync.dma_start(out=gate_row[0:1, :], in_=rw[0].rearrange("r o -> o r"))
        load("q", qT)
        load("do", doT)
        load("qm", qm)
        load("dom", dom)

        identity = sb("identity", [P, P], F32)
        make_identity(nc, identity[:])
        turned = psum.tile([P, PACK, P], F32, name="turned", tag="bank7")
        for t in range(PACK):
            nc.tensor.transpose(turned[:, t, :], gate_row[:, t:R:PACK], identity[:])
        nc.vector.tensor_scalar(out=neg_gate[:], in0=turned[:, :, 0], scalar1=-1.0, scalar2=None, op0=ALU.mult)

        windows = [sb("window%d" % j, [P, T], F32) for j in range(PACK)]
        for j in range(PACK):
            nc.vector.memset(windows[j][:], 0.0)

        codes = {name: sb("codes_" + name, [P, 512], U32) for name in FORMATS}
        scales = {name: sb("scales_" + name, [P, 512], U8) for name in FORMATS}
        half_width = HALF * PACK
        laid_c = sb("laid_c", [P, N * PACK], BF16)
        own_bytes = (("q", 0), ("q", 1), ("do", 0), ("ds", 0), ("pw", 0), ("qm", 0), ("dom", 1))
        laid = {key: sb("laid_%s%d" % key, [P, half_width], BF16)[:] for key in own_bytes}
        neg_pw_flat = sb("neg_pw", [P, PACK * N], F32)
        neg_pw = neg_pw_flat[:].rearrange("p (h t s) -> p h t s", h=2, t=PACK)
        straddle = neg_pw_flat[:, 4 * HALF : 8 * HALF].bitcast(BF16).rearrange("p (t w) -> p t w", t=2)
        late_do = straddle[:, :, HALF : HALF + P * PACK]
        stage = sb("stage", [P, 2 * half_width], BF16)
        laid["dom", 0] = stage[:, 3 * half_width // 4 : 7 * half_width // 4]
        laid["ds", 1] = laid["qm", 1] = stage[:, 0:half_width]
        laid["pw", 1] = stage[:, half_width : 2 * half_width]

        def quantize(name, h, first=0, count=2):
            cols = slice(h * HALF + P * first, h * HALF + P * (first + count))
            nc.vector.quantize_mx(
                out=codes[name][:, cols].bitcast(FORMATS[name]), scales=scales[name][:, cols],
                in_=laid[name, h][:, PACK * P * first : PACK * P * (first + count)],
            )

        def deal(copy, name, h, places=slice(0, P)):
            dst = laid[name, h].rearrange("p (t m j) -> p m j t", t=2, j=PACK)
            src = raw[name][:].rearrange("p j (m t) -> p m j t", t=PACK)
            copy(out=dst[:, places], in_=src[:, places, :, 2 * h : 2 * h + 2])

        def mx(out, stat, tile_index, mov, slots, start, stop):
            cols = slice(P * tile_index, P * (tile_index + 1))
            nc.tensor.matmul_mx(
                out=out,
                lhsT=codes[stat][:, cols].bitcast(FORMATS[stat]),
                lhsT_scale=scales[stat][:, cols],
                rhs=codes[mov][:, slots].bitcast(FORMATS[mov]),
                rhs_scale=scales[mov][:, slots],
                start=start,
                stop=stop,
            )

        whole = slice(0, N)
        halves = (slice(0, HALF), slice(HALF, N))
        c_lanes = laid_c[:].rearrange("p (s j) -> p s j", j=PACK)
        for j in range(PACK - 1):
            nc.vector.tensor_copy(out=c_lanes[:, :, j], in_=pool_planes[j][:].indirect(offsets[:]))
        for h in range(2):
            nc.vector.tensor_copy(out=c_lanes[:, halves[h], PACK - 1], in_=pool_planes[PACK - 1][:].indirect(list_halves[h]))
        for h in range(2):
            nc.vector.quantize_mx(
                out=codes["c"][:, halves[h]].bitcast(E4M3), scales=scales["c"][:, halves[h]],
                in_=laid_c[:, h * half_width : (h + 1) * half_width],
            )
        deal(nc.vector.tensor_copy, "q", 0)
        for t in range(2):
            deal(nc.vector.tensor_copy, "q", 1, slice(t * P // 2, (t + 1) * P // 2))
            quantize("q", 0, t, 1)
        quantize("q", 1)
        deal(nc.vector.tensor_copy, "do", 0)
        nc.vector.tensor_copy(
            out=late_do.rearrange("p t (m j) -> p m j t", j=PACK),
            in_=raw["do"][:].rearrange("p j (m t) -> p m j t", t=PACK)[:, :, :, 2:4],
        )
        quantize("do", 0)

        def bank(name, index, width):
            return psum.tile([P, width], F32, name=name, tag="bank%d" % index)

        score = [bank("score%d" % t, t, N) for t in range(PACK)]
        dprob = [bank("dprob%d" % t, PACK + t, N) for t in range(PACK)]
        prob = [sb("prob%d" % t, [P, N], F32) for t in range(PACK)]
        for t in range(PACK):
            mx(score[t][:], "q", t, "c", whole, True, True)
        for t in range(PACK):
            nc.scalar.activation(out=prob[t][:], in_=score[t][:], func=ACT.Sigmoid)

        def gate_product(engine, t, h):
            out, in_, factor = neg_pw[:, h, t, :], prob[t][:, halves[h]], neg_gate[:, t : t + 1]
            if engine is nc.scalar:
                engine.activation(out=out, in_=in_, func=ACT.Copy, scale=factor)
            else:
                engine.tensor_scalar(out=out, in0=in_, scalar1=factor, scalar2=0.0, op0=ALU.mult, op1=ALU.add)

        def gpsimd_round(out, in_):
            nc.gpsimd.tensor_scalar(out=out, in0=in_, scalar1=1.0, scalar2=0.0, op0=ALU.mult, op1=ALU.add)

        neg_dq = sb("neg_dq", [P, PACK, N], F32)
        gate_product(nc.vector, 0, 0)
        for t in (2, 3):
            cols = slice(P * t, P * (t + 1))
            nc.vector.quantize_mx(out=codes["do"][:, cols].bitcast(E5M2), scales=scales["do"][:, cols], in_=late_do[:, t - 2, :])
        for t in range(PACK):
            mx(dprob[t][:], "do", t, "c", whole, True, True)
        for t in (1, 2, 3):
            gate_product(nc.scalar, t, 0)
        for t in range(PACK):
            gate_product(nc.gpsimd, t, 1)
        for t in range(PACK):
            nc.vector.scalar_tensor_tensor(
                out=neg_dq[:, t, :], in0=prob[t][:], scalar=1.0, in1=dprob[t][:], op0=ALU.subtract, op1=ALU.mult
            )

        def runs(ap):
            return ap.rearrange("p t (c i) -> p c t i", i=4)

        def woven(ap):
            return ap.rearrange("p (c i t) -> p c t i", i=4, t=PACK)

        def weave_ds(h):
            nc.vector.tensor_tensor(
                out=woven(laid["ds", h]), in0=runs(neg_dq[:, :, halves[h]]), in1=runs(neg_pw[:, h]), op=ALU.mult
            )

        def products(planes, h, first, last):
            grads = {j: bank("grad%d%d" % (j, h), PACK * h + j, HALF) for j in planes}
            for stat, mov in (first, last):
                for j in planes:
                    mx(grads[j][:], stat, j, mov, halves[h], stat == first[0], stat == last[0])
            return grads

        def evict(copy, grads, j, h):
            copy(out=grad_sb[j, h][:], in_=grads[j][:])

        by_keys, by_values = ("qm", "ds"), ("dom", "pw")
        out_rows = out_0.rearrange("(p j) t -> j p t", j=PACK)
        grad_sb = {(j, h): sb("grad_sb%d%d" % (j, h), [P, HALF], F32) for j in range(PACK) for h in range(2)}

        def scatter_half(j, h):
            window = windows[j][:].indirect(list_halves[h])
            if h == 1 and j < 2:
                nc.vector.tensor_copy(out=window, in_=grad_sb[j, h][:])
            else:
                nc.scalar.activation(out=window, in_=grad_sb[j, h][:], func=ACT.Copy)

        def store(j):
            nc.sync.dma_start(out=out_rows[j], in_=windows[j][:])

        deal(nc.scalar.copy, "qm", 0)
        nc.scalar.activation(out=woven(laid["pw", 0]), in_=runs(neg_pw[:, 0]), func=ACT.Copy, scale=-1.0)
        for h in range(2):
            deal(nc.scalar.copy, "dom", h)
        weave_ds(0)
        for name in ("qm", "ds", "pw"):
            quantize(name, 0)
        for t in range(2):
            quantize("dom", 0, t, 1)
        first_low = products((0, 1), 0, by_keys, by_values)
        for j in (0, 1):
            evict(nc.scalar.copy, first_low, j, 0)
        for j in (0, 1):
            scatter_half(j, 0)
        weave_ds(1)
        nc.vector.tensor_scalar(
            out=woven(laid["pw", 1]), in0=runs(neg_pw[:, 1]), scalar1=-1.0, scalar2=None, op0=ALU.mult
        )
        quantize("ds", 1)
        quantize("pw", 1)
        second_low = products((0, 1), 1, by_keys, by_values)
        deal(nc.vector.tensor_copy, "qm", 1)
        quantize("dom", 1)
        quantize("qm", 1)
        first_high = products((2, 3), 0, by_values, by_keys)
        second_high = products((2, 3), 1, by_values, by_keys)
        for j in (0, 1):
            evict(nc.vector.tensor_copy, second_low, j, 1)
        scatter_half(0, 1)
        store(0)
        for j in (2, 3):
            evict(nc.vector.tensor_copy, second_high, j, 1)
        scatter_half(1, 1)
        store(1)
        for j in (2, 3):
            evict(nc.scalar.copy, first_high, j, 0)
        for j in (2, 3):
            scatter_half(j, 0)
        for j in (2, 3):
            scatter_half(j, 1)
            store(j)

        pairs = sb("pairs", [P, 2, T * 2], BF16, tag="codes_qm")

        def pair_words(lo, hi):
            return pairs[:, :, 2 * lo : 2 * hi]

        def pair_lanes(j, lo, hi):
            return pair_words(lo, hi)[:, j // 2, :].rearrange("p (t e) -> p t e", e=2)

        def round_lane(copy, j, lo, hi):
            copy(out=pair_lanes(j, lo, hi)[:, :, j % 2], in_=windows[j][:, lo:hi])

        round_lane(gpsimd_round, 0, BESIDE, T - HANDOVER)
        gpsimd_round(
            out=pair_lanes(0, T - HANDOVER, T),
            in_=windows[0][:, T - HANDOVER : T].unsqueeze(2).to_broadcast([P, HANDOVER, 2]),
        )
        round_lane(nc.vector.tensor_copy, 0, 0, BESIDE)
        round_lane(nc.vector.tensor_copy, 1, 0, BESIDE)
        round_lane(nc.vector.tensor_copy, 1, BESIDE, T)
        round_lane(nc.vector.tensor_copy, 2, HANDED, T)
        round_lane(nc.scalar.copy, 2, SPLIT, HANDED)
        round_lane(nc.vector.tensor_copy, 2, *VECTOR_CHUNKS[0])
        lo, hi = 1536 - HANDOVER // 2, 1536 + HANDOVER // 2
        nc.vector.tensor_copy(
            out=pair_lanes(2, lo, hi), in_=windows[2][:, lo:hi].unsqueeze(2).to_broadcast([P, HANDOVER, 2])
        )
        round_lane(nc.vector.tensor_copy, 2, *VECTOR_CHUNKS[1])

        chunks = VECTOR_CHUNKS + SCALAR_CHUNKS
        out_laid = {c: sb("out_laid%d" % c[0], [P, (c[1] - c[0]) * PACK], BF16) for c in chunks}
        out_codes = sb("out_codes", [P, T], U32)
        out_scales = sb("out_scales", [P, QUARTER], U8)
        words_dram = out_1[0].rearrange("p t l -> p (t l)").bitcast(I32)

        def weave_pairs(copy, c):
            src = pair_words(*c).bitcast(F32).rearrange("p u t -> p t u")
            copy(out=out_laid[c][:].bitcast(F32).rearrange("p (t u) -> p t u", u=2), in_=src)

        def quantize_out(c):
            lo = c[0]
            for hi in range(c[0] + P, c[1] + 1, P):
                if hi % 256 == 0 or hi == c[1]:
                    quarter, col = divmod(lo, QUARTER)
                    nc.vector.quantize_mx(
                        out=out_codes[:, lo:hi].bitcast(E4M3),
                        scales=out_scales[4 * quarter : P, col : col + hi - lo],
                        in_=out_laid[c][:, PACK * (lo - c[0]) : PACK * (hi - c[0])],
                    )
                    if hi in STORE_STARTS:
                        first = STORE_STARTS[hi]
                        nc.sync.dma_start(out=words_dram[:, first:hi], in_=out_codes[:, first:hi].bitcast(I32))
                    lo = hi

        for c in VECTOR_CHUNKS:
            round_lane(nc.vector.tensor_copy, 3, *c)
        for lo, hi in ((SPLIT, 1536), (1536, T)):
            round_lane(nc.scalar.copy, 3, lo, hi)
        for c in VECTOR_CHUNKS:
            weave_pairs(nc.vector.tensor_copy, c)
        for c in SCALAR_CHUNKS:
            weave_pairs(nc.scalar.copy, c)
        for c in chunks:
            quantize_out(c)
        for queue, quad in zip((nc.scalar, nc.scalar, nc.sync, nc.scalar), (0, 2, 1, 3)):
            queue.dma_start(
                out=out_2[0, 4 * quad : 4 * quad + 4, :].bitcast(I32).rearrange("f (u c) -> u f c", u=PACK),
                in_=out_scales[32 * quad : 32 * quad + 16, :].bitcast(I32),
            )
